import numpy as np
import ml_dtypes


def mxq(x, axis, fmt="e4m3"):
    dtype, down = {"e4m3": (ml_dtypes.float8_e4m3fn, 7), "e5m2": (ml_dtypes.float8_e5m2, 14)}[fmt]
    v = np.moveaxis(np.asarray(x, np.float32).astype(ml_dtypes.bfloat16).astype(np.float64), axis, -1)
    blocks = v.reshape(v.shape[:-1] + (-1, 32))
    amax = np.abs(blocks).max(-1, keepdims=True)
    byte = np.maximum(np.where(amax > 0, np.frexp(amax)[1] - 1 + 127, 0) - down, 1)
    scale = np.exp2(byte - 127.0)
    codes = (blocks / scale).astype(np.float32).astype(dtype).astype(np.float64)
    return np.moveaxis((codes * scale).reshape(v.shape), -1, axis)


WIDE = False


def mx_kscale(k):
    if not WIDE:
        return np.ones(k)
    levels = np.array([10, -10, 5, -5, 0])
    if k % 512:
        return np.exp2(np.random.permutation(np.resize(levels, k // 32))).repeat(32)
    a = np.empty((k // 512, 16))
    for p in range(k // 512):
        a[p, :8] = np.random.permutation(np.resize(levels, 8))
        for g in range(8):
            far = levels[np.abs(levels - a[p, g]) >= 10]
            a[p, g + 8] = far[np.random.randint(len(far))]
    return np.exp2(a.ravel()).repeat(32)


def f64(x):
    return np.asarray(x).astype(np.float64)


def striped8(idx):
    return np.concatenate([v.reshape(-1, 16).T for v in idx]).astype(np.uint16)


def unstriped8(offs):
    return np.stack([offs[16 * g:16 * g + 16].T.reshape(-1) for g in range(8)]).astype(np.int64)


K, M, T, S = 1536, 512, 2048, 512


def setup_inputs():
    n = np.random.standard_normal
    s = mx_kscale(K)[:, None]
    return {
        "xT": (n((K, T)) * s).astype(np.float32),
        "w": (n((K, M)) / np.sqrt(K) / s).astype(np.float32),
        "wgt": np.repeat(np.random.uniform(0.5, 2.0, (8, S)), 16, axis=0).astype(np.float32),
        "r": (n((512, 512))).astype(np.float32),
        "offs": striped8(np.stack([np.random.permutation(T)[:S] for _ in range(8)])),
    }


def reference(xT, w, wgt, r, offs):
    idx = unstriped8(offs)
    group = np.arange(K) % 512 // 64
    xg = f64(wgt)[np.arange(K) // 4 % 128] * f64(xT)[np.arange(K)[:, None], idx[group]]
    xT_ = mxq(xg, 0, "e4m3")
    w_ = mxq(f64(w), 0, "e4m3")
    y = xT_.T @ w_
    return f64(r) + y

@@ -1,0 +1,115 @@
+from contextlib import ExitStack
+
+import concourse.mybir as mybir
+
+K, M, T, S = 1536, 512, 2048, 512
+FLOPS = 2 * K * M * S
+
+F32 = mybir.dt.float32
+BF16 = mybir.dt.bfloat16
+U32 = mybir.dt.uint32
+U16 = mybir.dt.uint16
+U8 = mybir.dt.uint8
+FP8X4 = mybir.dt.float8_e4m3fn_x4
+MULT = mybir.AluOpType.mult
+ADD = mybir.AluOpType.add
+
+P = 128
+PACK = 4
+K_PASS = P * PACK
+PASSES = K // K_PASS
+HALF = S // 2
+N_HALF = M // 2
+
+
+def interleave(copy, out, src):
+    copy(out=out.rearrange("p (c j) -> p c j", j=PACK), in_=src.rearrange("p j c -> p c j"))
+
+
+def interleave4(copy, out, src):
+    copy(
+        out=out.rearrange("p (c i j) -> p c j i", i=4, j=PACK),
+        in_=src.rearrange("p j (c i) -> p c j i", i=4),
+    )
+
+
+def tile_list_heads_tm_res_kernel(tc, xT, w, wgt, r, offs, out):
+    nc = tc.nc
+    with ExitStack() as ctx:
+        keep = ctx.enter_context(tc.tile_pool(name="keep", bufs=1))
+        psum = ctx.enter_context(tc.psum_pool(name="psum", bufs=1))
+
+        offsets = keep.tile([P, S // 16], U16, name="offsets")
+        wgt_sb = keep.tile([P, S], F32, name="wgt_sb")
+        x_sb = [[keep.tile([P, T], F32, name=f"x{a}{i}") for i in range(PACK)] for a in range(PASSES)]
+        w_sb = [keep.tile([P, PACK * M], F32, name=f"w{a}") for a in range(PASSES)]
+        r_sb = [keep.tile([P, M], F32, name=f"r{b}") for b in range(S // P)]
+
+        for a in range(PASSES):
+            x_rows = xT[a * K_PASS : (a + 1) * K_PASS, :].rearrange("(p j) t -> p j t", j=PACK)
+            for i in range(PACK):
+                queue = nc.scalar if i % 2 else nc.sync
+                queue.dma_start(out=x_sb[a][i][:], in_=x_rows[:, i, :])
+                if a == 0 and i == 0:
+                    nc.sync.dma_start(offsets[:], offs)
+                    nc.sync.dma_start(out=wgt_sb[:], in_=wgt)
+        for a in range(PASSES):
+            nc.sync.dma_start(
+                out=w_sb[a][:],
+                in_=w[a * K_PASS : (a + 1) * K_PASS, :].rearrange("(p j) n -> p (j n)", j=PACK),
+            )
+        for b in range(S // P):
+            nc.sync.dma_start(out=r_sb[b][:], in_=r[b * P : (b + 1) * P, :])
+
+        acc = [[psum.tile([P, N_HALF], F32, name=f"acc{b}{g}") for g in range(2)] for b in range(S // P)]
+        x_codes = [[keep.tile([P, HALF], U32, name=f"xcodes{a}{h}", align_bytes=64) for h in range(2)] for a in range(PASSES)]
+        x_scales = [[keep.tile([P, HALF], U8, name=f"xscales{a}{h}", align_bytes=64) for h in range(2)] for a in range(PASSES)]
+
+        for a in range(PASSES):
+            last = a == PASSES - 1
+            picked = [keep.tile([P, PACK, HALF], F32, name=f"picked{a}{h}") for h in range(2)]
+            x_bf = [keep.tile([P, HALF * PACK], BF16, name=f"xbf{a}{h}", align_bytes=64) for h in range(2)]
+            for i in range(PACK):
+                for h in range(2):
+                    nc.vector.tensor_tensor(
+                        picked[h][:, i, :],
+                        x_sb[a][i][:].indirect(offsets[:, h * HALF // 16 : (h + 1) * HALF // 16]),
+                        wgt_sb[:, h * HALF : (h + 1) * HALF],
+                        MULT,
+                    )
+            interleave(nc.scalar.copy, x_bf[0][:], picked[0][:])
+            interleave(nc.vector.tensor_copy if last else nc.scalar.copy, x_bf[1][:], picked[1][:])
+            for h in range(2):
+                nc.vector.quantize_mx(out=x_codes[a][h][:].bitcast(FP8X4), scales=x_scales[a][h][:], in_=x_bf[h][:])
+
+        for a in range(PASSES):
+            w_rows = w_sb[a][:].rearrange("p (j n) -> p j n", j=PACK)
+            w_bf = [keep.tile([P, N_HALF * PACK], BF16, name=f"wbf{a}{g}", align_bytes=64) for g in range(2)]
+            w_codes = [keep.tile([P, N_HALF], U32, name=f"wcodes{a}{g}", align_bytes=64) for g in range(2)]
+            w_scales = [keep.tile([P, N_HALF], U8, name=f"wscales{a}{g}", align_bytes=64) for g in range(2)]
+            for g in range(2):
+                interleave4(nc.scalar.copy if g else nc.vector.tensor_copy, w_bf[g][:], w_rows[:, :, g * N_HALF : (g + 1) * N_HALF])
+            for g in range(2):
+                nc.vector.quantize_mx(out=w_codes[g][:].bitcast(FP8X4), scales=w_scales[g][:], in_=w_bf[g][:])
+                for b in range(S // P):
+                    h, cols = b // 2, slice(b % 2 * P, (b % 2 + 1) * P)
+                    nc.tensor.matmul_mx(
+                        out=acc[b][g][:],
+                        lhsT=x_codes[a][h][:, cols].bitcast(FP8X4),
+                        lhsT_scale=x_scales[a][h][:, cols],
+                        rhs=w_codes[g][:].bitcast(FP8X4),
+                        rhs_scale=w_scales[g][:],
+                        start=a == 0,
+                        stop=a == PASSES - 1,
+                    )
+
+        raw = keep.tile([P, N_HALF], F32, name="raw")
+        for b, g in ((0, 0), (1, 0), (2, 0), (0, 1), (3, 0), (1, 1), (2, 1), (3, 1)):
+            cols = slice(g * N_HALF, (g + 1) * N_HALF)
+            result = keep.tile([P, N_HALF], F32, name=f"result{b}{g}")
+            if (b, g) == (3, 0):
+                nc.scalar.copy(out=raw[:], in_=acc[b][g][:])
+                nc.gpsimd.tensor_tensor(result[:], raw[:], r_sb[b][:, cols], ADD)
+            else:
+                nc.vector.tensor_tensor(result[:], acc[b][g][:], r_sb[b][:, cols], ADD)
+            nc.sync.dma_start(out=out[b * P : (b + 1) * P, cols], in_=result[:])

@@ -37,60 +37,124 @@ def tile_list_heads_tm_res_kernel(tc, xT, w, wgt, r, offs, out):
     nc = tc.nc
     with ExitStack() as ctx:
         keep = ctx.enter_context(tc.tile_pool(name="keep", bufs=1))
+        ring = ctx.enter_context(tc.tile_pool(name="ring", bufs=2))
+        work = ctx.enter_context(tc.tile_pool(name="work", bufs=1))
         psum = ctx.enter_context(tc.psum_pool(name="psum", bufs=1))
 
         offsets = keep.tile([P, S // 16], U16, name="offsets")
-        wgt_sb = keep.tile([P, S], F32, name="wgt_sb")
-        x_sb = [[keep.tile([P, T], F32, name=f"x{a}{i}") for i in range(PACK)] for a in range(PASSES)]
-        w_sb = [keep.tile([P, PACK * M], F32, name=f"w{a}") for a in range(PASSES)]
-        r_sb = [keep.tile([P, M], F32, name=f"r{b}") for b in range(S // P)]
+        wgt_sb = keep.tile([P, S], F32, name="wgt_sb", align_bytes=64)
+        wgt_rows = keep.tile([P, S], F32, name="wgt_rows", align_bytes=64)
+        wgt_turned = keep.tile([P, S], F32, name="wgt_turned", align_bytes=64)
+        wgt_spread = keep.tile([P, S], F32, name="wgt_spread", align_bytes=64)
+        nc.vector.memset(wgt_rows[:], 0.0)
 
+        window = [[None] * PACK for a in range(PASSES)]
         for a in range(PASSES):
-            x_rows = xT[a * K_PASS : (a + 1) * K_PASS, :].rearrange("(p j) t -> p j t", j=PACK)
-            for i in range(PACK):
-                queue = nc.scalar if i % 2 else nc.sync
-                queue.dma_start(out=x_sb[a][i][:], in_=x_rows[:, i, :])
+            x_rows = xT[a * K_PASS : (a + 1) * K_PASS, :].rearrange("(p j) t -> p (j t)", j=PACK)
+            for i in range(0, PACK, 2):
+                if a > 0 and i == 2:
+                    for e in (i, i + 1):
+                        window[a][e] = keep.tile([P, T], F32, name=f"x{a}{e}")
+                        nc.sync.dma_start(out=window[a][e][:], in_=x_rows[:, e * T : (e + 1) * T])
+                else:
+                    window[a][i] = keep.tile([P, 2 * T], F32, name=f"x{a}{i}")
+                    nc.sync.dma_start(out=window[a][i][:], in_=x_rows[:, i * T : (i + 2) * T])
                 if a == 0 and i == 0:
                     nc.sync.dma_start(offsets[:], offs)
-                    nc.sync.dma_start(out=wgt_sb[:], in_=wgt)
-        for a in range(PASSES):
+                    nc.sync.dma_start(out=wgt_rows[0:P:16, :], in_=wgt[0:P:16, :])
+        w_sb = [keep.tile([P, PACK * M], F32, name=f"w{a}") for a in range(PASSES - 1)]
+        for a in range(PASSES - 1):
             nc.sync.dma_start(
                 out=w_sb[a][:],
                 in_=w[a * K_PASS : (a + 1) * K_PASS, :].rearrange("(p j) n -> p (j n)", j=PACK),
             )
+        w_last = [keep.tile([P, 2 * M], F32, name=f"wlast{e}") for e in range(2)]
+        for e in range(2):
+            nc.sync.dma_start(
+                out=w_last[e][:],
+                in_=w[K - K_PASS :, :].rearrange("(p j) n -> p (j n)", j=PACK)[:, 2 * e * M : 2 * (e + 1) * M],
+            )
+        r_sb = [keep.tile([P, M], F32, name=f"r{b}") for b in range(S // P)]
         for b in range(S // P):
             nc.sync.dma_start(out=r_sb[b][:], in_=r[b * P : (b + 1) * P, :])
 
+        nc.vector.transpose(wgt_turned[:], wgt_rows[:])
+        nc.vector.tensor_copy(
+            out=wgt_spread[:].rearrange("p (c i) -> p c i", i=16),
+            in_=wgt_turned[:].rearrange("p (c i) -> p c i", i=16)[:, :, 0:1].to_broadcast([P, S // 16, 16]),
+        )
+        nc.vector.transpose(wgt_sb[:], wgt_spread[:])
+
         acc = [[psum.tile([P, N_HALF], F32, name=f"acc{b}{g}") for g in range(2)] for b in range(S // P)]
-        x_codes = [[keep.tile([P, HALF], U32, name=f"xcodes{a}{h}", align_bytes=64) for h in range(2)] for a in range(PASSES)]
+        x_codes = [[keep.tile([P, HALF], U32, name=f"xcodes{a}{h}", align_bytes=64) for h in range(2)] for a in range(PASSES - 1)]
+        x_codes.append([work.tile([P, HALF], U32, name=f"xcodes_last{h}", offset=h * HALF * 4, align_bytes=64) for h in range(2)])
         x_scales = [[keep.tile([P, HALF], U8, name=f"xscales{a}{h}", align_bytes=64) for h in range(2)] for a in range(PASSES)]
+        picked = [[ring.tile([P, PACK, HALF], F32, name=f"picked{h}") for h in range(2)] for a in range(PASSES)]
+        x_bf = [[ring.tile([P, HALF * PACK], BF16, name=f"xbf{h}", align_bytes=64) for h in range(2)] for a in range(PASSES)]
 
-        for a in range(PASSES):
-            last = a == PASSES - 1
-            picked = [keep.tile([P, PACK, HALF], F32, name=f"picked{a}{h}") for h in range(2)]
-            x_bf = [keep.tile([P, HALF * PACK], BF16, name=f"xbf{a}{h}", align_bytes=64) for h in range(2)]
-            for i in range(PACK):
-                for h in range(2):
-                    nc.vector.tensor_tensor(
-                        picked[h][:, i, :],
-                        x_sb[a][i][:].indirect(offsets[:, h * HALF // 16 : (h + 1) * HALF // 16]),
-                        wgt_sb[:, h * HALF : (h + 1) * HALF],
-                        MULT,
-                    )
-            interleave(nc.scalar.copy, x_bf[0][:], picked[0][:])
-            interleave(nc.vector.tensor_copy if last else nc.scalar.copy, x_bf[1][:], picked[1][:])
+        def unpair(copy, a, i, c0, c1):
+            if window[a][i] is None:
+                window[a][i] = ring.tile([P, T], F32, name="second")
+            copy(out=window[a][i][:, c0:c1], in_=window[a][i - 1][:, T + c0 : T + c1])
+
+        def gather(a, i):
             for h in range(2):
-                nc.vector.quantize_mx(out=x_codes[a][h][:].bitcast(FP8X4), scales=x_scales[a][h][:], in_=x_bf[h][:])
+                nc.vector.tensor_tensor(
+                    picked[a][h][:, i, :],
+                    window[a][i][:].indirect(offsets[:, h * HALF // 16 : (h + 1) * HALF // 16]),
+                    wgt_sb[:, h * HALF : (h + 1) * HALF],
+                    MULT,
+                )
+
+        def weave_x(copy, a, h):
+            interleave4(copy, x_bf[a][h][:], picked[a][h][:])
+
+        def quantize_x(a, h):
+            nc.vector.quantize_mx(out=x_codes[a][h][:].bitcast(FP8X4), scales=x_scales[a][h][:], in_=x_bf[a][h][:])
+
+        on_scalar, on_vector = nc.scalar.copy, nc.vector.tensor_copy
+        share = 1536
+        for a in range(PASSES):
+            unpair(on_scalar, a, 1, 0, share if a == PASSES - 1 else T)
+            gather(a, 0)
+            if a == PASSES - 1:
+                unpair(on_vector, a, 1, share, T)
+            gather(a, 1)
+            if a == 0:
+                unpair(on_scalar, a, 3, 0, share)
+            gather(a, 2)
+            if a == 0:
+                unpair(on_vector, a, 3, share, T)
+            gather(a, 3)
+            weave_x(on_scalar, a, 0)
+            weave_x(on_vector, a, 1)
+            if a < PASSES - 1:
+                quantize_x(a, 1)
+                quantize_x(a, 0)
 
         for a in range(PASSES):
-            w_rows = w_sb[a][:].rearrange("p (j n) -> p j n", j=PACK)
-            w_bf = [keep.tile([P, N_HALF * PACK], BF16, name=f"wbf{a}{g}", align_bytes=64) for g in range(2)]
+            w_bf = [keep.tile([P, N_HALF * PACK], BF16, name=f"wbf{a}{g}", align_bytes=64) if a or g else None for g in range(2)]
+            if a == 0:
+                w_bf[0] = work.tile([P, N_HALF * PACK], BF16, name="wbf_first", offset=0, align_bytes=64)
             w_codes = [keep.tile([P, N_HALF], U32, name=f"wcodes{a}{g}", align_bytes=64) for g in range(2)]
             w_scales = [keep.tile([P, N_HALF], U8, name=f"wscales{a}{g}", align_bytes=64) for g in range(2)]
-            for g in range(2):
-                interleave4(nc.scalar.copy if g else nc.vector.tensor_copy, w_bf[g][:], w_rows[:, :, g * N_HALF : (g + 1) * N_HALF])
+            if a < PASSES - 1:
+                w_rows = w_sb[a][:].rearrange("p (j n) -> p j n", j=PACK)
+                for g in range(2):
+                    interleave4(on_scalar if g else on_vector, w_bf[g][:], w_rows[:, :, g * N_HALF : (g + 1) * N_HALF])
+            else:
+                for e in range(2):
+                    w_rows = w_last[e][:].rearrange("p (j n) -> p j n", j=2)
+                    for g in range(2):
+                        (on_scalar if g else on_vector)(
+                            out=w_bf[g][:].rearrange("p (c j) -> p c j", j=PACK)[:, :, 2 * e : 2 * e + 2],
+                            in_=w_rows[:, :, g * N_HALF : (g + 1) * N_HALF].rearrange("p j c -> p c j"),
+                        )
             for g in range(2):
                 nc.vector.quantize_mx(out=w_codes[g][:].bitcast(FP8X4), scales=w_scales[g][:], in_=w_bf[g][:])
+                if (a, g) == (0, 0):
+                    quantize_x(PASSES - 1, 1)
+                    quantize_x(PASSES - 1, 0)
                 for b in range(S // P):
                     h, cols = b // 2, slice(b % 2 * P, (b % 2 + 1) * P)
                     nc.tensor.matmul_mx(

@@ -89,7 +89,7 @@ def tile_list_heads_tm_res_kernel(tc, xT, w, wgt, r, offs, out):
         x_codes = [[keep.tile([P, HALF], U32, name=f"xcodes{a}{h}", align_bytes=64) for h in range(2)] for a in range(PASSES - 1)]
         x_codes.append([work.tile([P, HALF], U32, name=f"xcodes_last{h}", offset=h * HALF * 4, align_bytes=64) for h in range(2)])
         x_scales = [[keep.tile([P, HALF], U8, name=f"xscales{a}{h}", align_bytes=64) for h in range(2)] for a in range(PASSES)]
-        picked = [[ring.tile([P, PACK, HALF], F32, name=f"picked{h}") for h in range(2)] for a in range(PASSES)]
+        picked = [ring.tile([P, PACK, S], F32, name="picked") for a in range(PASSES)]
         x_bf = [[ring.tile([P, HALF * PACK], BF16, name=f"xbf{h}", align_bytes=64) for h in range(2)] for a in range(PASSES)]
 
         def unpair(copy, a, i, c0, c1):
@@ -98,16 +98,13 @@ def tile_list_heads_tm_res_kernel(tc, xT, w, wgt, r, offs, out):
             copy(out=window[a][i][:, c0:c1], in_=window[a][i - 1][:, T + c0 : T + c1])
 
         def gather(a, i):
-            for h in range(2):
-                nc.vector.tensor_tensor(
-                    picked[a][h][:, i, :],
-                    window[a][i][:].indirect(offsets[:, h * HALF // 16 : (h + 1) * HALF // 16]),
-                    wgt_sb[:, h * HALF : (h + 1) * HALF],
-                    MULT,
-                )
+            parts = 2 if window[a][i].shape[1] > T or i == PACK - 1 else 1
+            for h in range(parts):
+                c0, c1 = h * S // parts, (h + 1) * S // parts
+                nc.vector.tensor_tensor(picked[a][:, i, c0:c1], window[a][i][:].indirect(offsets[:, c0 // 16 : c1 // 16]), wgt_sb[:, c0:c1], MULT)
 
         def weave_x(copy, a, h):
-            interleave4(copy, x_bf[a][h][:], picked[a][h][:])
+            interleave4(copy, x_bf[a][h][:], picked[a][:, :, h * HALF : (h + 1) * HALF])
 
         def quantize_x(a, h):
             nc.vector.quantize_mx(out=x_codes[a][h][:].bitcast(FP8X4), scales=x_scales[a][h][:], in_=x_bf[a][h][:])
@@ -145,17 +142,22 @@ def tile_list_heads_tm_res_kernel(tc, xT, w, wgt, r, offs, out):
             else:
                 for e in range(2):
                     w_rows = w_last[e][:].rearrange("p (j n) -> p j n", j=2)
-                    for g in range(2):
-                        (on_scalar if g else on_vector)(
-                            out=w_bf[g][:].rearrange("p (c j) -> p c j", j=PACK)[:, :, 2 * e : 2 * e + 2],
-                            in_=w_rows[:, :, g * N_HALF : (g + 1) * N_HALF].rearrange("p j c -> p c j"),
+                    if e == 0:
+                        shares = ((on_vector, 0, 0, N_HALF), (on_scalar, 1, 0, N_HALF))
+                    else:
+                        shares = ((on_vector, 0, 0, 192), (on_scalar, 0, 192, N_HALF), (on_vector, 1, 0, 128), (on_scalar, 1, 128, N_HALF))
+                    for copy, g, c0, c1 in shares:
+                        copy(
+                            out=w_bf[g][:].rearrange("p (c j) -> p c j", j=PACK)[:, c0:c1, 2 * e : 2 * e + 2],
+                            in_=w_rows[:, :, g * N_HALF + c0 : g * N_HALF + c1].rearrange("p j c -> p c j"),
                         )
             for g in range(2):
                 nc.vector.quantize_mx(out=w_codes[g][:].bitcast(FP8X4), scales=w_scales[g][:], in_=w_bf[g][:])
                 if (a, g) == (0, 0):
                     quantize_x(PASSES - 1, 1)
                     quantize_x(PASSES - 1, 0)
-                for b in range(S // P):
+            for b, g in ((0, 0), (2, 0), (0, 1), (1, 0), (1, 1), (2, 1), (3, 0), (3, 1)):
+                if True:
                     h, cols = b // 2, slice(b % 2 * P, (b % 2 + 1) * P)
                     nc.tensor.matmul_mx(
                         out=acc[b][g][:],
@@ -167,13 +169,16 @@ def tile_list_heads_tm_res_kernel(tc, xT, w, wgt, r, offs, out):
                         stop=a == PASSES - 1,
                     )
 
+        result = [keep.tile([P, M], F32, name=f"result{b}") for b in range(S // P)]
         raw = keep.tile([P, N_HALF], F32, name="raw")
-        for b, g in ((0, 0), (1, 0), (2, 0), (0, 1), (3, 0), (1, 1), (2, 1), (3, 1)):
-            cols = slice(g * N_HALF, (g + 1) * N_HALF)
-            result = keep.tile([P, N_HALF], F32, name=f"result{b}{g}")
-            if (b, g) == (3, 0):
-                nc.scalar.copy(out=raw[:], in_=acc[b][g][:])
-                nc.gpsimd.tensor_tensor(result[:], raw[:], r_sb[b][:, cols], ADD)
-            else:
-                nc.vector.tensor_tensor(result[:], acc[b][g][:], r_sb[b][:, cols], ADD)
-            nc.sync.dma_start(out=out[b * P : (b + 1) * P, cols], in_=result[:])
+        nc.scalar.copy(out=raw[:], in_=acc[2][0][:])
+        nc.gpsimd.tensor_tensor(result[2][:, :N_HALF], raw[:], r_sb[2][:, :N_HALF], ADD)
+        for b in range(S // P):
+            for g in range(2):
+                cols = slice(g * N_HALF, (g + 1) * N_HALF)
+                if (b, g) != (2, 0):
+                    nc.vector.tensor_tensor(result[b][:, cols], acc[b][g][:], r_sb[b][:, cols], ADD)
+                if b < 2:
+                    nc.sync.dma_start(out=out[b * P : (b + 1) * P, cols], in_=result[b][:, cols])
+            if b >= 2:
+                nc.sync.dma_start(out=out[b * P : (b + 1) * P, :], in_=result[b][:])

@@ -85,7 +85,11 @@ def tile_list_heads_tm_res_kernel(tc, xT, w, wgt, r, offs, out):
         )
         nc.vector.transpose(wgt_sb[:], wgt_spread[:])
 
-        acc = [[psum.tile([P, N_HALF], F32, name=f"acc{b}{g}") for g in range(2)] for b in range(S // P)]
+        pieces = ((0, 0, 128), (0, 128, 256), (2, 0, 256), (1, 0, 256), (0, 256, 512), (1, 256, 512), (2, 256, 512), (3, 0, 256), (3, 256, 512))
+        acc = {piece: psum.tile([P, piece[2] - piece[1]], F32, name=f"acc{piece[0]}_{piece[1]}")[:] for piece in pieces[:-2]}
+        acc_last = psum.tile([P, M], F32, name="acc_last")
+        for piece in pieces[-2:]:
+            acc[piece] = acc_last[:, piece[1] : piece[2]]
         x_codes = [[keep.tile([P, HALF], U32, name=f"xcodes{a}{h}", align_bytes=64) for h in range(2)] for a in range(PASSES - 1)]
         x_codes.append([work.tile([P, HALF], U32, name=f"xcodes_last{h}", offset=h * HALF * 4, align_bytes=64) for h in range(2)])
         x_scales = [[keep.tile([P, HALF], U8, name=f"xscales{a}{h}", align_bytes=64) for h in range(2)] for a in range(PASSES)]
@@ -124,7 +128,11 @@ def tile_list_heads_tm_res_kernel(tc, xT, w, wgt, r, offs, out):
                 unpair(on_vector, a, 3, share, T)
             gather(a, 3)
             weave_x(on_scalar, a, 0)
-            weave_x(on_vector, a, 1)
+            if a < PASSES - 1:
+                weave_x(on_vector, a, 1)
+            else:
+                interleave4(on_vector, x_bf[a][1][:, : 128 * PACK], picked[a][:, :, HALF : HALF + 128])
+                interleave4(on_scalar, x_bf[a][1][:, 128 * PACK :], picked[a][:, :, HALF + 128 :])
             if a < PASSES - 1:
                 quantize_x(a, 1)
                 quantize_x(a, 0)
@@ -145,40 +153,44 @@ def tile_list_heads_tm_res_kernel(tc, xT, w, wgt, r, offs, out):
                     if e == 0:
                         shares = ((on_vector, 0, 0, N_HALF), (on_scalar, 1, 0, N_HALF))
                     else:
-                        shares = ((on_vector, 0, 0, 192), (on_scalar, 0, 192, N_HALF), (on_vector, 1, 0, 128), (on_scalar, 1, 128, N_HALF))
+                        shares = ((on_vector, 0, 0, 128), (on_scalar, 0, 128, N_HALF), (on_vector, 1, 0, 128), (on_scalar, 1, 128, N_HALF))
                     for copy, g, c0, c1 in shares:
                         copy(
                             out=w_bf[g][:].rearrange("p (c j) -> p c j", j=PACK)[:, c0:c1, 2 * e : 2 * e + 2],
                             in_=w_rows[:, :, g * N_HALF + c0 : g * N_HALF + c1].rearrange("p j c -> p c j"),
                         )
             for g in range(2):
-                nc.vector.quantize_mx(out=w_codes[g][:].bitcast(FP8X4), scales=w_scales[g][:], in_=w_bf[g][:])
+                parts = 2 if (a, g) == (PASSES - 1, 0) else 1
+                for q in range(parts):
+                    c0, c1 = q * N_HALF // parts, (q + 1) * N_HALF // parts
+                    nc.vector.quantize_mx(out=w_codes[g][:, c0:c1].bitcast(FP8X4), scales=w_scales[g][:, c0:c1], in_=w_bf[g][:, c0 * PACK : c1 * PACK])
                 if (a, g) == (0, 0):
                     quantize_x(PASSES - 1, 1)
                     quantize_x(PASSES - 1, 0)
-            for b, g in ((0, 0), (2, 0), (0, 1), (1, 0), (1, 1), (2, 1), (3, 0), (3, 1)):
-                if True:
-                    h, cols = b // 2, slice(b % 2 * P, (b % 2 + 1) * P)
-                    nc.tensor.matmul_mx(
-                        out=acc[b][g][:],
-                        lhsT=x_codes[a][h][:, cols].bitcast(FP8X4),
-                        lhsT_scale=x_scales[a][h][:, cols],
-                        rhs=w_codes[g][:].bitcast(FP8X4),
-                        rhs_scale=w_scales[g][:],
-                        start=a == 0,
-                        stop=a == PASSES - 1,
-                    )
+            for b, c0, c1 in pieces:
+                h, tok = b // 2, slice(b % 2 * P, (b % 2 + 1) * P)
+                g = c0 // N_HALF
+                cols = slice(c0 - g * N_HALF, c1 - g * N_HALF)
+                nc.tensor.matmul_mx(
+                    out=acc[b, c0, c1],
+                    lhsT=x_codes[a][h][:, tok].bitcast(FP8X4),
+                    lhsT_scale=x_scales[a][h][:, tok],
+                    rhs=w_codes[g][:, cols].bitcast(FP8X4),
+                    rhs_scale=w_scales[g][:, cols],
+                    start=a == 0 and (b, c0, c1) != pieces[-1],
+                    stop=a == PASSES - 1 and (b, c0, c1) != pieces[-2],
+                )
 
         result = [keep.tile([P, M], F32, name=f"result{b}") for b in range(S // P)]
         raw = keep.tile([P, N_HALF], F32, name="raw")
-        nc.scalar.copy(out=raw[:], in_=acc[2][0][:])
+        nc.scalar.copy(out=raw[:], in_=acc[2, 0, 256])
         nc.gpsimd.tensor_tensor(result[2][:, :N_HALF], raw[:], r_sb[2][:, :N_HALF], ADD)
-        for b in range(S // P):
-            for g in range(2):
-                cols = slice(g * N_HALF, (g + 1) * N_HALF)
-                if (b, g) != (2, 0):
-                    nc.vector.tensor_tensor(result[b][:, cols], acc[b][g][:], r_sb[b][:, cols], ADD)
+        for b, c0, c1 in pieces[:-2]:
+            if (b, c0) != (2, 0):
+                nc.vector.tensor_tensor(result[b][:, c0:c1], acc[b, c0, c1], r_sb[b][:, c0:c1], ADD)
                 if b < 2:
-                    nc.sync.dma_start(out=out[b * P : (b + 1) * P, cols], in_=result[b][:, cols])
-            if b >= 2:
-                nc.sync.dma_start(out=out[b * P : (b + 1) * P, :], in_=result[b][:])
+                    nc.sync.dma_start(out=out[b * P : (b + 1) * P, c0:c1], in_=result[b][:, c0:c1])
+                else:
+                    nc.sync.dma_start(out=out[b * P : (b + 1) * P, :], in_=result[b][:])
+        nc.vector.tensor_tensor(result[3][:], acc_last[:], r_sb[3][:], ADD)
+        nc.sync.dma_start(out=out[3 * P :, :], in_=result[3][:])

@@ -48,11 +48,12 @@ def tile_list_heads_tm_res_kernel(tc, xT, w, wgt, r, offs, out):
         wgt_spread = keep.tile([P, S], F32, name="wgt_spread", align_bytes=64)
         nc.vector.memset(wgt_rows[:], 0.0)
 
+        nc.sync.dma_start(offsets[:], offs)
         window = [[None] * PACK for a in range(PASSES)]
         for a in range(PASSES):
             x_rows = xT[a * K_PASS : (a + 1) * K_PASS, :].rearrange("(p j) t -> p (j t)", j=PACK)
             for i in range(0, PACK, 2):
-                if a > 0 and i == 2:
+                if a > 1 and i == 2:
                     for e in (i, i + 1):
                         window[a][e] = keep.tile([P, T], F32, name=f"x{a}{e}")
                         nc.sync.dma_start(out=window[a][e][:], in_=x_rows[:, e * T : (e + 1) * T])
@@ -60,7 +61,6 @@ def tile_list_heads_tm_res_kernel(tc, xT, w, wgt, r, offs, out):
                     window[a][i] = keep.tile([P, 2 * T], F32, name=f"x{a}{i}")
                     nc.sync.dma_start(out=window[a][i][:], in_=x_rows[:, i * T : (i + 2) * T])
                 if a == 0 and i == 0:
-                    nc.sync.dma_start(offsets[:], offs)
                     nc.sync.dma_start(out=wgt_rows[0:P:16, :], in_=wgt[0:P:16, :])
         w_sb = [keep.tile([P, PACK * M], F32, name=f"w{a}") for a in range(PASSES - 1)]
         for a in range(PASSES - 1):
@@ -121,10 +121,10 @@ def tile_list_heads_tm_res_kernel(tc, xT, w, wgt, r, offs, out):
             if a == PASSES - 1:
                 unpair(on_vector, a, 1, share, T)
             gather(a, 1)
-            if a == 0:
+            if a < PASSES - 1:
                 unpair(on_scalar, a, 3, 0, share)
             gather(a, 2)
-            if a == 0:
+            if a < PASSES - 1:
                 unpair(on_vector, a, 3, share, T)
             gather(a, 3)
             weave_x(on_scalar, a, 0)

@@ -18,30 +18,39 @@ P = 128
 PACK = 4
 K_PASS = P * PACK
 PASSES = K // K_PASS
+LAST = PASSES - 1
+GROUP = 16
 HALF = S // 2
 N_HALF = M // 2
+NARROW = N_HALF // 2
+BLOCKS = S // P
+
+SCALAR_SHARE_PLANE3 = 1408
+SCALAR_SHARE_LAST_PASS = 1664
+VECTOR_WEAVE_LAST = HALF // 2
+
+GPSIMD_PIECE = (2, 0, N_HALF)
+OWN_BANK = ((0, 0, NARROW), (0, NARROW, N_HALF), GPSIMD_PIECE, (1, 0, N_HALF), (0, N_HALF, M), (1, N_HALF, M), (2, N_HALF, M))
+SHARED_BANK = ((BLOCKS - 1, 0, N_HALF), (BLOCKS - 1, N_HALF, M))
 
 
-def interleave(copy, out, src):
-    copy(out=out.rearrange("p (c j) -> p c j", j=PACK), in_=src.rearrange("p j c -> p c j"))
-
-
-def interleave4(copy, out, src):
+def weave(copy, out, planes):
     copy(
         out=out.rearrange("p (c i j) -> p c j i", i=4, j=PACK),
-        in_=src.rearrange("p j (c i) -> p c j i", i=4),
+        in_=planes.rearrange("p j (c i) -> p c j i", i=4),
     )
 
 
 def tile_list_heads_tm_res_kernel(tc, xT, w, wgt, r, offs, out):
     nc = tc.nc
+    on_scalar, on_vector = nc.scalar.copy, nc.vector.tensor_copy
     with ExitStack() as ctx:
         keep = ctx.enter_context(tc.tile_pool(name="keep", bufs=1))
         ring = ctx.enter_context(tc.tile_pool(name="ring", bufs=2))
         work = ctx.enter_context(tc.tile_pool(name="work", bufs=1))
         psum = ctx.enter_context(tc.psum_pool(name="psum", bufs=1))
 
-        offsets = keep.tile([P, S // 16], U16, name="offsets")
+        offsets = keep.tile([P, S // GROUP], U16, name="offsets")
         wgt_sb = keep.tile([P, S], F32, name="wgt_sb", align_bytes=64)
         wgt_rows = keep.tile([P, S], F32, name="wgt_rows", align_bytes=64)
         wgt_turned = keep.tile([P, S], F32, name="wgt_turned", align_bytes=64)
@@ -49,21 +58,22 @@ def tile_list_heads_tm_res_kernel(tc, xT, w, wgt, r, offs, out):
         nc.vector.memset(wgt_rows[:], 0.0)
 
         nc.sync.dma_start(offsets[:], offs)
+
         window = [[None] * PACK for a in range(PASSES)]
         for a in range(PASSES):
             x_rows = xT[a * K_PASS : (a + 1) * K_PASS, :].rearrange("(p j) t -> p (j t)", j=PACK)
             for i in range(0, PACK, 2):
-                if a > 1 and i == 2:
+                if (a, i) == (LAST, PACK - 2):
                     for e in (i, i + 1):
                         window[a][e] = keep.tile([P, T], F32, name=f"x{a}{e}")
                         nc.sync.dma_start(out=window[a][e][:], in_=x_rows[:, e * T : (e + 1) * T])
                 else:
                     window[a][i] = keep.tile([P, 2 * T], F32, name=f"x{a}{i}")
                     nc.sync.dma_start(out=window[a][i][:], in_=x_rows[:, i * T : (i + 2) * T])
-                if a == 0 and i == 0:
-                    nc.sync.dma_start(out=wgt_rows[0:P:16, :], in_=wgt[0:P:16, :])
-        w_sb = [keep.tile([P, PACK * M], F32, name=f"w{a}") for a in range(PASSES - 1)]
-        for a in range(PASSES - 1):
+                if (a, i) == (0, 0):
+                    nc.sync.dma_start(out=wgt_rows[0:P:GROUP, :], in_=wgt[0:P:GROUP, :])
+        w_sb = [keep.tile([P, PACK * M], F32, name=f"w{a}") for a in range(LAST)]
+        for a in range(LAST):
             nc.sync.dma_start(
                 out=w_sb[a][:],
                 in_=w[a * K_PASS : (a + 1) * K_PASS, :].rearrange("(p j) n -> p (j n)", j=PACK),
@@ -74,23 +84,23 @@ def tile_list_heads_tm_res_kernel(tc, xT, w, wgt, r, offs, out):
                 out=w_last[e][:],
                 in_=w[K - K_PASS :, :].rearrange("(p j) n -> p (j n)", j=PACK)[:, 2 * e * M : 2 * (e + 1) * M],
             )
-        r_sb = [keep.tile([P, M], F32, name=f"r{b}") for b in range(S // P)]
-        for b in range(S // P):
+        r_sb = [keep.tile([P, M], F32, name=f"r{b}") for b in range(BLOCKS)]
+        for b in range(BLOCKS):
             nc.sync.dma_start(out=r_sb[b][:], in_=r[b * P : (b + 1) * P, :])
 
         nc.vector.transpose(wgt_turned[:], wgt_rows[:])
         nc.vector.tensor_copy(
-            out=wgt_spread[:].rearrange("p (c i) -> p c i", i=16),
-            in_=wgt_turned[:].rearrange("p (c i) -> p c i", i=16)[:, :, 0:1].to_broadcast([P, S // 16, 16]),
+            out=wgt_spread[:].rearrange("p (c i) -> p c i", i=GROUP),
+            in_=wgt_turned[:].rearrange("p (c i) -> p c i", i=GROUP)[:, :, 0:1].to_broadcast([P, S // GROUP, GROUP]),
         )
         nc.vector.transpose(wgt_sb[:], wgt_spread[:])
 
-        pieces = ((0, 0, 128), (0, 128, 256), (2, 0, 256), (1, 0, 256), (0, 256, 512), (1, 256, 512), (2, 256, 512), (3, 0, 256), (3, 256, 512))
-        acc = {piece: psum.tile([P, piece[2] - piece[1]], F32, name=f"acc{piece[0]}_{piece[1]}")[:] for piece in pieces[:-2]}
+        acc = {piece: psum.tile([P, piece[2] - piece[1]], F32, name=f"acc{piece[0]}_{piece[1]}")[:] for piece in OWN_BANK}
         acc_last = psum.tile([P, M], F32, name="acc_last")
-        for piece in pieces[-2:]:
+        for piece in SHARED_BANK:
             acc[piece] = acc_last[:, piece[1] : piece[2]]
-        x_codes = [[keep.tile([P, HALF], U32, name=f"xcodes{a}{h}", align_bytes=64) for h in range(2)] for a in range(PASSES - 1)]
+
+        x_codes = [[keep.tile([P, HALF], U32, name=f"xcodes{a}{h}", align_bytes=64) for h in range(2)] for a in range(LAST)]
         x_codes.append([work.tile([P, HALF], U32, name=f"xcodes_last{h}", offset=h * HALF * 4, align_bytes=64) for h in range(2)])
         x_scales = [[keep.tile([P, HALF], U8, name=f"xscales{a}{h}", align_bytes=64) for h in range(2)] for a in range(PASSES)]
         picked = [ring.tile([P, PACK, S], F32, name="picked") for a in range(PASSES)]
@@ -105,37 +115,39 @@ def tile_list_heads_tm_res_kernel(tc, xT, w, wgt, r, offs, out):
             parts = 2 if window[a][i].shape[1] > T or i == PACK - 1 else 1
             for h in range(parts):
                 c0, c1 = h * S // parts, (h + 1) * S // parts
-                nc.vector.tensor_tensor(picked[a][:, i, c0:c1], window[a][i][:].indirect(offsets[:, c0 // 16 : c1 // 16]), wgt_sb[:, c0:c1], MULT)
+                nc.vector.tensor_tensor(
+                    picked[a][:, i, c0:c1],
+                    window[a][i][:].indirect(offsets[:, c0 // GROUP : c1 // GROUP]),
+                    wgt_sb[:, c0:c1],
+                    MULT,
+                )
 
-        def weave_x(copy, a, h):
-            interleave4(copy, x_bf[a][h][:], picked[a][:, :, h * HALF : (h + 1) * HALF])
+        def weave_x(copy, a, h, c0, c1):
+            weave(copy, x_bf[a][h][:, c0 * PACK : c1 * PACK], picked[a][:, :, h * HALF + c0 : h * HALF + c1])
 
-        def quantize_x(a, h):
-            nc.vector.quantize_mx(out=x_codes[a][h][:].bitcast(FP8X4), scales=x_scales[a][h][:], in_=x_bf[a][h][:])
+        def quantize_x(a):
+            for h in (1, 0):
+                nc.vector.quantize_mx(out=x_codes[a][h][:].bitcast(FP8X4), scales=x_scales[a][h][:], in_=x_bf[a][h][:])
 
-        on_scalar, on_vector = nc.scalar.copy, nc.vector.tensor_copy
-        share = 1536
-        for a in range(PASSES):
-            unpair(on_scalar, a, 1, 0, share if a == PASSES - 1 else T)
+        for a in range(LAST):
+            unpair(on_scalar, a, 1, 0, T)
             gather(a, 0)
-            if a == PASSES - 1:
-                unpair(on_vector, a, 1, share, T)
             gather(a, 1)
-            if a < PASSES - 1:
-                unpair(on_scalar, a, 3, 0, share)
+            unpair(on_scalar, a, 3, 0, SCALAR_SHARE_PLANE3)
             gather(a, 2)
-            if a < PASSES - 1:
-                unpair(on_vector, a, 3, share, T)
+            unpair(on_vector, a, 3, SCALAR_SHARE_PLANE3, T)
             gather(a, 3)
-            weave_x(on_scalar, a, 0)
-            if a < PASSES - 1:
-                weave_x(on_vector, a, 1)
-            else:
-                interleave4(on_vector, x_bf[a][1][:, : 128 * PACK], picked[a][:, :, HALF : HALF + 128])
-                interleave4(on_scalar, x_bf[a][1][:, 128 * PACK :], picked[a][:, :, HALF + 128 :])
-            if a < PASSES - 1:
-                quantize_x(a, 1)
-                quantize_x(a, 0)
+            weave_x(on_scalar, a, 0, 0, HALF)
+            weave_x(on_vector, a, 1, 0, HALF)
+            quantize_x(a)
+        unpair(on_scalar, LAST, 1, 0, SCALAR_SHARE_LAST_PASS)
+        gather(LAST, 0)
+        unpair(on_vector, LAST, 1, SCALAR_SHARE_LAST_PASS, T)
+        for i in range(1, PACK):
+            gather(LAST, i)
+        weave_x(on_scalar, LAST, 0, 0, HALF)
+        weave_x(on_vector, LAST, 1, 0, VECTOR_WEAVE_LAST)
+        weave_x(on_scalar, LAST, 1, VECTOR_WEAVE_LAST, HALF)
 
         for a in range(PASSES):
             w_bf = [keep.tile([P, N_HALF * PACK], BF16, name=f"wbf{a}{g}", align_bytes=64) if a or g else None for g in range(2)]
@@ -143,54 +155,58 @@ def tile_list_heads_tm_res_kernel(tc, xT, w, wgt, r, offs, out):
                 w_bf[0] = work.tile([P, N_HALF * PACK], BF16, name="wbf_first", offset=0, align_bytes=64)
             w_codes = [keep.tile([P, N_HALF], U32, name=f"wcodes{a}{g}", align_bytes=64) for g in range(2)]
             w_scales = [keep.tile([P, N_HALF], U8, name=f"wscales{a}{g}", align_bytes=64) for g in range(2)]
-            if a < PASSES - 1:
-                w_rows = w_sb[a][:].rearrange("p (j n) -> p j n", j=PACK)
-                for g in range(2):
-                    interleave4(on_scalar if g else on_vector, w_bf[g][:], w_rows[:, :, g * N_HALF : (g + 1) * N_HALF])
+            if a < LAST:
+                w_planes = w_sb[a][:].rearrange("p (j n) -> p j n", j=PACK)
+                for g, copy in enumerate((on_vector, on_scalar)):
+                    weave(copy, w_bf[g][:], w_planes[:, :, g * N_HALF : (g + 1) * N_HALF])
             else:
-                for e in range(2):
-                    w_rows = w_last[e][:].rearrange("p (j n) -> p j n", j=2)
-                    if e == 0:
-                        shares = ((on_vector, 0, 0, N_HALF), (on_scalar, 1, 0, N_HALF))
-                    else:
-                        shares = ((on_vector, 0, 0, 128), (on_scalar, 0, 128, N_HALF), (on_vector, 1, 0, 128), (on_scalar, 1, 128, N_HALF))
+                first_load = ((on_vector, 0, 0, N_HALF), (on_scalar, 1, 0, N_HALF))
+                second_load = tuple(
+                    (copy, g, c0, c0 + NARROW) for g in range(2) for copy, c0 in ((on_vector, 0), (on_scalar, NARROW))
+                )
+                for e, shares in enumerate((first_load, second_load)):
+                    w_planes = w_last[e][:].rearrange("p (j n) -> p j n", j=2)
                     for copy, g, c0, c1 in shares:
                         copy(
                             out=w_bf[g][:].rearrange("p (c j) -> p c j", j=PACK)[:, c0:c1, 2 * e : 2 * e + 2],
-                            in_=w_rows[:, :, g * N_HALF + c0 : g * N_HALF + c1].rearrange("p j c -> p c j"),
+                            in_=w_planes[:, :, g * N_HALF + c0 : g * N_HALF + c1].rearrange("p j c -> p c j"),
                         )
             for g in range(2):
-                parts = 2 if (a, g) == (PASSES - 1, 0) else 1
-                for q in range(parts):
-                    c0, c1 = q * N_HALF // parts, (q + 1) * N_HALF // parts
-                    nc.vector.quantize_mx(out=w_codes[g][:, c0:c1].bitcast(FP8X4), scales=w_scales[g][:, c0:c1], in_=w_bf[g][:, c0 * PACK : c1 * PACK])
+                width = NARROW if (a, g) == (LAST, 0) else N_HALF
+                for c0 in range(0, N_HALF, width):
+                    nc.vector.quantize_mx(
+                        out=w_codes[g][:, c0 : c0 + width].bitcast(FP8X4),
+                        scales=w_scales[g][:, c0 : c0 + width],
+                        in_=w_bf[g][:, c0 * PACK : (c0 + width) * PACK],
+                    )
                 if (a, g) == (0, 0):
-                    quantize_x(PASSES - 1, 1)
-                    quantize_x(PASSES - 1, 0)
-            for b, c0, c1 in pieces:
-                h, tok = b // 2, slice(b % 2 * P, (b % 2 + 1) * P)
+                    quantize_x(LAST)
+            for piece in OWN_BANK + SHARED_BANK:
+                b, c0, c1 = piece
+                h, tokens = b // 2, slice(b % 2 * P, (b % 2 + 1) * P)
                 g = c0 // N_HALF
                 cols = slice(c0 - g * N_HALF, c1 - g * N_HALF)
                 nc.tensor.matmul_mx(
-                    out=acc[b, c0, c1],
-                    lhsT=x_codes[a][h][:, tok].bitcast(FP8X4),
-                    lhsT_scale=x_scales[a][h][:, tok],
+                    out=acc[piece],
+                    lhsT=x_codes[a][h][:, tokens].bitcast(FP8X4),
+                    lhsT_scale=x_scales[a][h][:, tokens],
                     rhs=w_codes[g][:, cols].bitcast(FP8X4),
                     rhs_scale=w_scales[g][:, cols],
-                    start=a == 0 and (b, c0, c1) != pieces[-1],
-                    stop=a == PASSES - 1 and (b, c0, c1) != pieces[-2],
+                    start=a == 0 and piece != SHARED_BANK[1],
+                    stop=a == LAST and piece != SHARED_BANK[0],
                 )
 
-        result = [keep.tile([P, M], F32, name=f"result{b}") for b in range(S // P)]
+        result = [keep.tile([P, M], F32, name=f"result{b}") for b in range(BLOCKS)]
         raw = keep.tile([P, N_HALF], F32, name="raw")
-        nc.scalar.copy(out=raw[:], in_=acc[2, 0, 256])
-        nc.gpsimd.tensor_tensor(result[2][:, :N_HALF], raw[:], r_sb[2][:, :N_HALF], ADD)
-        for b, c0, c1 in pieces[:-2]:
-            if (b, c0) != (2, 0):
-                nc.vector.tensor_tensor(result[b][:, c0:c1], acc[b, c0, c1], r_sb[b][:, c0:c1], ADD)
-                if b < 2:
-                    nc.sync.dma_start(out=out[b * P : (b + 1) * P, c0:c1], in_=result[b][:, c0:c1])
-                else:
-                    nc.sync.dma_start(out=out[b * P : (b + 1) * P, :], in_=result[b][:])
-        nc.vector.tensor_tensor(result[3][:], acc_last[:], r_sb[3][:], ADD)
-        nc.sync.dma_start(out=out[3 * P :, :], in_=result[3][:])
+        b, c0, c1 = GPSIMD_PIECE
+        nc.scalar.copy(out=raw[:], in_=acc[GPSIMD_PIECE])
+        nc.gpsimd.tensor_tensor(result[b][:, c0:c1], raw[:], r_sb[b][:, c0:c1], ADD)
+        for piece in OWN_BANK:
+            if piece != GPSIMD_PIECE:
+                b, c0, c1 = piece
+                nc.vector.tensor_tensor(result[b][:, c0:c1], acc[piece], r_sb[b][:, c0:c1], ADD)
+                stored = slice(0, M) if b == GPSIMD_PIECE[0] else slice(c0, c1)
+                nc.sync.dma_start(out=out[b * P : (b + 1) * P, stored], in_=result[b][:, stored])
+        b = BLOCKS - 1
+        nc.vector.tensor_tensor(result[b][:], acc_last[:], r_sb[b][:], ADD)
+        nc.sync.dma_start(out=out[b * P :, :], in_=result[b][:])

@@ -23,20 +23,26 @@ GROUP = 16
 HALF = S // 2
 N_HALF = M // 2
 NARROW = N_HALF // 2
-BLOCKS = S // P
 
 SCALAR_SHARE_PLANE3 = 1408
-SCALAR_SHARE_LAST_PASS = 1664
-VECTOR_WEAVE_LAST = HALF // 2
 
-GPSIMD_PIECE = (2, 0, N_HALF)
-OWN_BANK = ((0, 0, NARROW), (0, NARROW, N_HALF), GPSIMD_PIECE, (1, 0, N_HALF), (0, N_HALF, M), (1, N_HALF, M), (2, N_HALF, M))
-SHARED_BANK = ((BLOCKS - 1, 0, N_HALF), (BLOCKS - 1, N_HALF, M))
+VECTOR_EXTRA_W1 = 64
+
+GPSIMD_PIECE = (1, 0, 0, N_HALF)
+OWN_BANK = ((0, 0, 0, N_HALF), (0, 1, 0, N_HALF), GPSIMD_PIECE, (0, 0, N_HALF, M), (0, 1, N_HALF, M), (1, 0, N_HALF, M))
+SHARED_BANK = ((1, 1, 0, N_HALF), (1, 1, N_HALF, M))
 
 
 def weave(copy, out, planes):
     copy(
         out=out.rearrange("p (c i j) -> p c j i", i=4, j=PACK),
+        in_=planes.rearrange("p j (c i) -> p c j i", i=4),
+    )
+
+
+def weave_pair(copy, out, j, planes):
+    copy(
+        out=out.rearrange("p (c i j) -> p c j i", i=4, j=PACK)[:, :, j : j + 2, :],
         in_=planes.rearrange("p j (c i) -> p c j i", i=4),
     )
 
@@ -63,7 +69,7 @@ def tile_list_heads_tm_res_kernel(tc, xT, w, wgt, r, offs, out):
         for a in range(PASSES):
             x_rows = xT[a * K_PASS : (a + 1) * K_PASS, :].rearrange("(p j) t -> p (j t)", j=PACK)
             for i in range(0, PACK, 2):
-                if (a, i) == (LAST, PACK - 2):
+                if a == LAST:
                     for e in (i, i + 1):
                         window[a][e] = keep.tile([P, T], F32, name=f"x{a}{e}")
                         nc.sync.dma_start(out=window[a][e][:], in_=x_rows[:, e * T : (e + 1) * T])
@@ -72,21 +78,20 @@ def tile_list_heads_tm_res_kernel(tc, xT, w, wgt, r, offs, out):
                     nc.sync.dma_start(out=window[a][i][:], in_=x_rows[:, i * T : (i + 2) * T])
                 if (a, i) == (0, 0):
                     nc.sync.dma_start(out=wgt_rows[0:P:GROUP, :], in_=wgt[0:P:GROUP, :])
-        w_sb = [keep.tile([P, PACK * M], F32, name=f"w{a}") for a in range(LAST)]
+        w_rows = [w[a * K_PASS : (a + 1) * K_PASS, :].rearrange("(p j) n -> p (j n)", j=PACK) for a in range(PASSES)]
+        w_sb = [keep.tile([P, PACK * M], F32, name=f"w{a}") for a in range(PASSES)]
         for a in range(LAST):
-            nc.sync.dma_start(
-                out=w_sb[a][:],
-                in_=w[a * K_PASS : (a + 1) * K_PASS, :].rearrange("(p j) n -> p (j n)", j=PACK),
-            )
-        w_last = [keep.tile([P, 2 * M], F32, name=f"wlast{e}") for e in range(2)]
+            nc.sync.dma_start(out=w_sb[a][:], in_=w_rows[a])
+        for c0, c1 in ((0, 2 * M + N_HALF), (3 * M, 3 * M + N_HALF)):
+            nc.sync.dma_start(out=w_sb[LAST][:, c0:c1], in_=w_rows[LAST][:, c0:c1])
+        w_rest = keep.tile([P, 2, N_HALF], F32, name="w_rest")
+        nc.sync.dma_start(out=w_rest[:], in_=w_rows[LAST].rearrange("p (j n) -> p j n", j=PACK)[:, 2:, N_HALF:])
+        r_rows = [r[h * HALF : (h + 1) * HALF, :].rearrange("(q e) n -> q (e n)", e=2) for h in range(2)]
+        out_rows = [out[h * HALF : (h + 1) * HALF, :].rearrange("(q e) n -> q (e n)", e=2) for h in range(2)]
+        r_sb = [keep.tile([P, 2 * M], F32, name=f"r{h}") for h in range(2)]
+        nc.sync.dma_start(out=r_sb[0][:], in_=r_rows[0])
         for e in range(2):
-            nc.sync.dma_start(
-                out=w_last[e][:],
-                in_=w[K - K_PASS :, :].rearrange("(p j) n -> p (j n)", j=PACK)[:, 2 * e * M : 2 * (e + 1) * M],
-            )
-        r_sb = [keep.tile([P, M], F32, name=f"r{b}") for b in range(BLOCKS)]
-        for b in range(BLOCKS):
-            nc.sync.dma_start(out=r_sb[b][:], in_=r[b * P : (b + 1) * P, :])
+            nc.sync.dma_start(out=r_sb[1][:, e * M : (e + 1) * M], in_=r_rows[1][:, e * M : (e + 1) * M])
 
         nc.vector.transpose(wgt_turned[:], wgt_rows[:])
         nc.vector.tensor_copy(
@@ -95,13 +100,13 @@ def tile_list_heads_tm_res_kernel(tc, xT, w, wgt, r, offs, out):
         )
         nc.vector.transpose(wgt_sb[:], wgt_spread[:])
 
-        acc = {piece: psum.tile([P, piece[2] - piece[1]], F32, name=f"acc{piece[0]}_{piece[1]}")[:] for piece in OWN_BANK}
+        acc = {piece: psum.tile([P, piece[3] - piece[2]], F32, name="acc%d%d_%d" % piece[:3])[:] for piece in OWN_BANK}
         acc_last = psum.tile([P, M], F32, name="acc_last")
         for piece in SHARED_BANK:
-            acc[piece] = acc_last[:, piece[1] : piece[2]]
+            acc[piece] = acc_last[:, piece[2] : piece[3]]
 
         x_codes = [[keep.tile([P, HALF], U32, name=f"xcodes{a}{h}", align_bytes=64) for h in range(2)] for a in range(LAST)]
-        x_codes.append([work.tile([P, HALF], U32, name=f"xcodes_last{h}", offset=h * HALF * 4, align_bytes=64) for h in range(2)])
+        x_codes.append([keep.tile([P, HALF], U32, name="xcodes_last0", align_bytes=64), work.tile([P, HALF], U32, name="xcodes_last1", offset=0, align_bytes=64)])
         x_scales = [[keep.tile([P, HALF], U8, name=f"xscales{a}{h}", align_bytes=64) for h in range(2)] for a in range(PASSES)]
         picked = [ring.tile([P, PACK, S], F32, name="picked") for a in range(PASSES)]
         x_bf = [[ring.tile([P, HALF * PACK], BF16, name=f"xbf{h}", align_bytes=64) for h in range(2)] for a in range(PASSES)]
@@ -122,12 +127,14 @@ def tile_list_heads_tm_res_kernel(tc, xT, w, wgt, r, offs, out):
                     MULT,
                 )
 
-        def weave_x(copy, a, h, c0, c1):
-            weave(copy, x_bf[a][h][:, c0 * PACK : c1 * PACK], picked[a][:, :, h * HALF + c0 : h * HALF + c1])
+        def weave_x(copy, a, h, j0, j1):
+            copy(
+                out=x_bf[a][h][:].rearrange("p (e c u j) -> p c j u e", e=2, u=2, j=PACK)[:, :, j0:j1, :, :],
+                in_=picked[a][:, j0:j1, h * HALF : (h + 1) * HALF].rearrange("p j (c u e) -> p c j u e", u=2, e=2),
+            )
 
-        def quantize_x(a):
-            for h in (1, 0):
-                nc.vector.quantize_mx(out=x_codes[a][h][:].bitcast(FP8X4), scales=x_scales[a][h][:], in_=x_bf[a][h][:])
+        def quantize_x(a, h):
+            nc.vector.quantize_mx(out=x_codes[a][h][:].bitcast(FP8X4), scales=x_scales[a][h][:], in_=x_bf[a][h][:])
 
         for a in range(LAST):
             unpair(on_scalar, a, 1, 0, T)
@@ -137,17 +144,19 @@ def tile_list_heads_tm_res_kernel(tc, xT, w, wgt, r, offs, out):
             gather(a, 2)
             unpair(on_vector, a, 3, SCALAR_SHARE_PLANE3, T)
             gather(a, 3)
-            weave_x(on_scalar, a, 0, 0, HALF)
-            weave_x(on_vector, a, 1, 0, HALF)
-            quantize_x(a)
-        unpair(on_scalar, LAST, 1, 0, SCALAR_SHARE_LAST_PASS)
+            weave_x(on_scalar, a, 0, 0, PACK)
+            weave_x(on_scalar if a else on_vector, a, 1, 0, PACK)
+            quantize_x(a, 0)
+            quantize_x(a, 1)
         gather(LAST, 0)
-        unpair(on_vector, LAST, 1, SCALAR_SHARE_LAST_PASS, T)
-        for i in range(1, PACK):
-            gather(LAST, i)
-        weave_x(on_scalar, LAST, 0, 0, HALF)
-        weave_x(on_vector, LAST, 1, 0, VECTOR_WEAVE_LAST)
-        weave_x(on_scalar, LAST, 1, VECTOR_WEAVE_LAST, HALF)
+        gather(LAST, 1)
+        for h in range(2):
+            weave_x(on_scalar, LAST, h, 0, 2)
+        gather(LAST, 2)
+        gather(LAST, 3)
+        weave_x(on_scalar, LAST, 0, 2, PACK)
+        weave_x(on_scalar, LAST, 1, 2, PACK)
+        quantize_x(LAST, 0)
 
         for a in range(PASSES):
             w_bf = [keep.tile([P, N_HALF * PACK], BF16, name=f"wbf{a}{g}", align_bytes=64) if a or g else None for g in range(2)]
@@ -155,24 +164,22 @@ def tile_list_heads_tm_res_kernel(tc, xT, w, wgt, r, offs, out):
                 w_bf[0] = work.tile([P, N_HALF * PACK], BF16, name="wbf_first", offset=0, align_bytes=64)
             w_codes = [keep.tile([P, N_HALF], U32, name=f"wcodes{a}{g}", align_bytes=64) for g in range(2)]
             w_scales = [keep.tile([P, N_HALF], U8, name=f"wscales{a}{g}", align_bytes=64) for g in range(2)]
+            w_planes = w_sb[a][:].rearrange("p (j n) -> p j n", j=PACK)
+            width0 = N_HALF if a == 1 else NARROW
+            for c0 in range(0, N_HALF, width0):
+                weave(on_vector, w_bf[0][:, c0 * PACK : (c0 + width0) * PACK], w_planes[:, :, c0 : c0 + width0])
             if a < LAST:
-                w_planes = w_sb[a][:].rearrange("p (j n) -> p j n", j=PACK)
-                for g, copy in enumerate((on_vector, on_scalar)):
-                    weave(copy, w_bf[g][:], w_planes[:, :, g * N_HALF : (g + 1) * N_HALF])
+                extra = VECTOR_EXTRA_W1 * a
+                if extra:
+                    weave(on_vector, w_bf[1][:, : extra * PACK], w_planes[:, :, N_HALF : N_HALF + extra])
+                weave(on_scalar, w_bf[1][:, extra * PACK :], w_planes[:, :, N_HALF + extra :])
             else:
-                first_load = ((on_vector, 0, 0, N_HALF), (on_scalar, 1, 0, N_HALF))
-                second_load = tuple(
-                    (copy, g, c0, c0 + NARROW) for g in range(2) for copy, c0 in ((on_vector, 0), (on_scalar, NARROW))
-                )
-                for e, shares in enumerate((first_load, second_load)):
-                    w_planes = w_last[e][:].rearrange("p (j n) -> p j n", j=2)
-                    for copy, g, c0, c1 in shares:
-                        copy(
-                            out=w_bf[g][:].rearrange("p (c j) -> p c j", j=PACK)[:, c0:c1, 2 * e : 2 * e + 2],
-                            in_=w_planes[:, :, g * N_HALF + c0 : g * N_HALF + c1].rearrange("p j c -> p c j"),
-                        )
+                weave_pair(on_scalar, w_bf[1][:], 0, w_planes[:, 0:2, N_HALF:])
+                weave_pair(on_scalar, w_bf[1][:, NARROW * PACK :], 2, w_rest[:, :, NARROW:])
             for g in range(2):
-                width = NARROW if (a, g) == (LAST, 0) else N_HALF
+                width = width0 if g == 0 else N_HALF
+                if (a, g) == (LAST, 1):
+                    weave_pair(on_vector, w_bf[1][:, : NARROW * PACK], 2, w_rest[:, :, :NARROW])
                 for c0 in range(0, N_HALF, width):
                     nc.vector.quantize_mx(
                         out=w_codes[g][:, c0 : c0 + width].bitcast(FP8X4),
@@ -180,33 +187,40 @@ def tile_list_heads_tm_res_kernel(tc, xT, w, wgt, r, offs, out):
                         in_=w_bf[g][:, c0 * PACK : (c0 + width) * PACK],
                     )
                 if (a, g) == (0, 0):
-                    quantize_x(LAST)
-            for piece in OWN_BANK + SHARED_BANK:
-                b, c0, c1 = piece
-                h, tokens = b // 2, slice(b % 2 * P, (b % 2 + 1) * P)
+                    quantize_x(LAST, 1)
+            pieces = sorted(OWN_BANK + SHARED_BANK, key=lambda piece: piece[2] // N_HALF)
+            sweeps = [(piece, piece[2], piece[3]) for piece in pieces]
+            if a == 0:
+                sweeps = [
+                    (piece, c0, c0 + NARROW) for c0 in (0, NARROW) for piece in pieces if piece[2] <= c0 < piece[3]
+                ] + [sweep for sweep in sweeps if sweep[1] >= N_HALF]
+            for piece, c0, c1 in sweeps:
+                h, e = piece[:2]
                 g = c0 // N_HALF
+                tokens = slice(e * P, (e + 1) * P)
                 cols = slice(c0 - g * N_HALF, c1 - g * N_HALF)
                 nc.tensor.matmul_mx(
-                    out=acc[piece],
+                    out=acc[piece][:, c0 - piece[2] : c1 - piece[2]],
                     lhsT=x_codes[a][h][:, tokens].bitcast(FP8X4),
                     lhsT_scale=x_scales[a][h][:, tokens],
                     rhs=w_codes[g][:, cols].bitcast(FP8X4),
                     rhs_scale=w_scales[g][:, cols],
-                    start=a == 0 and piece != SHARED_BANK[1],
+                    start=a == 0 and c0 == piece[2] and piece != SHARED_BANK[1],
                     stop=a == LAST and piece != SHARED_BANK[0],
                 )
 
-        result = [keep.tile([P, M], F32, name=f"result{b}") for b in range(BLOCKS)]
+        result = [keep.tile([P, 2 * M], F32, name=f"result{h}") for h in range(2)]
         raw = keep.tile([P, N_HALF], F32, name="raw")
-        b, c0, c1 = GPSIMD_PIECE
+        h, e, c0, c1 = GPSIMD_PIECE
+        cols = slice(e * M + c0, e * M + c1)
         nc.scalar.copy(out=raw[:], in_=acc[GPSIMD_PIECE])
-        nc.gpsimd.tensor_tensor(result[b][:, c0:c1], raw[:], r_sb[b][:, c0:c1], ADD)
+        nc.gpsimd.tensor_tensor(result[h][:, cols], raw[:], r_sb[h][:, cols], ADD)
         for piece in OWN_BANK:
             if piece != GPSIMD_PIECE:
-                b, c0, c1 = piece
-                nc.vector.tensor_tensor(result[b][:, c0:c1], acc[piece], r_sb[b][:, c0:c1], ADD)
-                stored = slice(0, M) if b == GPSIMD_PIECE[0] else slice(c0, c1)
-                nc.sync.dma_start(out=out[b * P : (b + 1) * P, stored], in_=result[b][:, stored])
-        b = BLOCKS - 1
-        nc.vector.tensor_tensor(result[b][:], acc_last[:], r_sb[b][:], ADD)
-        nc.sync.dma_start(out=out[b * P :, :], in_=result[b][:])
+                h, e, c0, c1 = piece
+                cols = slice(e * M + c0, e * M + c1)
+                nc.vector.tensor_tensor(result[h][:, cols], acc[piece], r_sb[h][:, cols], ADD)
+                stored = slice(0, M) if h else cols
+                nc.sync.dma_start(out=out_rows[h][:, stored], in_=result[h][:, stored])
+        nc.vector.tensor_tensor(result[1][:, M:], acc_last[:], r_sb[1][:, M:], ADD)
+        nc.sync.dma_start(out=out_rows[1][:, M:], in_=result[1][:, M:])

@@ -23,6 +23,7 @@ GROUP = 16
 HALF = S // 2
 N_HALF = M // 2
 NARROW = N_HALF // 2
+BURST = 256
 
 SCALAR_SHARE_PLANE3 = 1408
 
@@ -56,9 +57,9 @@ def tile_list_heads_tm_res_kernel(tc, xT, w, wgt, r, offs, out):
         work = ctx.enter_context(tc.tile_pool(name="work", bufs=1))
         psum = ctx.enter_context(tc.psum_pool(name="psum", bufs=1))
 
-        offsets = keep.tile([P, S // GROUP], U16, name="offsets")
+        offsets = keep.tile([P, S // GROUP], U16, name="offsets", align_bytes=BURST)
         wgt_sb = keep.tile([P, S], F32, name="wgt_sb", align_bytes=64)
-        wgt_rows = keep.tile([P, S], F32, name="wgt_rows", align_bytes=64)
+        wgt_rows = keep.tile([P, S], F32, name="wgt_rows", align_bytes=BURST)
         wgt_turned = keep.tile([P, S], F32, name="wgt_turned", align_bytes=64)
         wgt_spread = keep.tile([P, S], F32, name="wgt_spread", align_bytes=64)
         nc.vector.memset(wgt_rows[:], 0.0)
@@ -71,24 +72,24 @@ def tile_list_heads_tm_res_kernel(tc, xT, w, wgt, r, offs, out):
             for i in range(0, PACK, 2):
                 if a == LAST:
                     for e in (i, i + 1):
-                        window[a][e] = keep.tile([P, T], F32, name=f"x{a}{e}")
+                        window[a][e] = keep.tile([P, T], F32, name=f"x{a}{e}", align_bytes=BURST)
                         nc.sync.dma_start(out=window[a][e][:], in_=x_rows[:, e * T : (e + 1) * T])
                 else:
-                    window[a][i] = keep.tile([P, 2 * T], F32, name=f"x{a}{i}")
+                    window[a][i] = keep.tile([P, 2 * T], F32, name=f"x{a}{i}", align_bytes=BURST)
                     nc.sync.dma_start(out=window[a][i][:], in_=x_rows[:, i * T : (i + 2) * T])
                 if (a, i) == (0, 0):
                     nc.sync.dma_start(out=wgt_rows[0:P:GROUP, :], in_=wgt[0:P:GROUP, :])
         w_rows = [w[a * K_PASS : (a + 1) * K_PASS, :].rearrange("(p j) n -> p (j n)", j=PACK) for a in range(PASSES)]
-        w_sb = [keep.tile([P, PACK * M], F32, name=f"w{a}") for a in range(PASSES)]
+        w_sb = [keep.tile([P, PACK * M], F32, name=f"w{a}", align_bytes=BURST) for a in range(PASSES)]
         for a in range(LAST):
             nc.sync.dma_start(out=w_sb[a][:], in_=w_rows[a])
         for c0, c1 in ((0, 2 * M + N_HALF), (3 * M, 3 * M + N_HALF)):
             nc.sync.dma_start(out=w_sb[LAST][:, c0:c1], in_=w_rows[LAST][:, c0:c1])
-        w_rest = keep.tile([P, 2, N_HALF], F32, name="w_rest")
+        w_rest = keep.tile([P, 2, N_HALF], F32, name="w_rest", align_bytes=BURST)
         nc.sync.dma_start(out=w_rest[:], in_=w_rows[LAST].rearrange("p (j n) -> p j n", j=PACK)[:, 2:, N_HALF:])
         r_rows = [r[h * HALF : (h + 1) * HALF, :].rearrange("(q e) n -> q (e n)", e=2) for h in range(2)]
         out_rows = [out[h * HALF : (h + 1) * HALF, :].rearrange("(q e) n -> q (e n)", e=2) for h in range(2)]
-        r_sb = [keep.tile([P, 2 * M], F32, name=f"r{h}") for h in range(2)]
+        r_sb = [keep.tile([P, 2 * M], F32, name=f"r{h}", align_bytes=BURST) for h in range(2)]
         nc.sync.dma_start(out=r_sb[0][:], in_=r_rows[0])
         for e in range(2):
             nc.sync.dma_start(out=r_sb[1][:, e * M : (e + 1) * M], in_=r_rows[1][:, e * M : (e + 1) * M])
@@ -209,7 +210,7 @@ def tile_list_heads_tm_res_kernel(tc, xT, w, wgt, r, offs, out):
                     stop=a == LAST and piece != SHARED_BANK[0],
                 )
 
-        result = [keep.tile([P, 2 * M], F32, name=f"result{h}") for h in range(2)]
+        result = [keep.tile([P, 2 * M], F32, name=f"result{h}", align_bytes=BURST) for h in range(2)]
         raw = keep.tile([P, N_HALF], F32, name="raw")
         h, e, c0, c1 = GPSIMD_PIECE
         cols = slice(e * M + c0, e * M + c1)

@@ -28,9 +28,10 @@ BURST = 256
 SCALAR_SHARE_PLANE3 = 1408
 
 VECTOR_EXTRA_W1 = 64
+VECTOR_LATE = 96
 
 GPSIMD_PIECE = (1, 0, 0, N_HALF)
-OWN_BANK = ((0, 0, 0, N_HALF), (0, 1, 0, N_HALF), GPSIMD_PIECE, (0, 0, N_HALF, M), (0, 1, N_HALF, M), (1, 0, N_HALF, M))
+OWN_BANK = ((0, 0, 0, N_HALF), GPSIMD_PIECE, (0, 1, 0, N_HALF), (0, 0, N_HALF, M), (0, 1, N_HALF, M), (1, 0, N_HALF, M))
 SHARED_BANK = ((1, 1, 0, N_HALF), (1, 1, N_HALF, M))
 
 
@@ -59,12 +60,10 @@ def tile_list_heads_tm_res_kernel(tc, xT, w, wgt, r, offs, out):
 
         offsets = keep.tile([P, S // GROUP], U16, name="offsets", align_bytes=BURST)
         wgt_sb = keep.tile([P, S], F32, name="wgt_sb", align_bytes=64)
-        wgt_rows = keep.tile([P, S], F32, name="wgt_rows", align_bytes=BURST)
-        wgt_turned = keep.tile([P, S], F32, name="wgt_turned", align_bytes=64)
+        wgt_rows = keep.tile([P, HALF], F32, name="wgt_rows", align_bytes=BURST)
+        wgt_turned = keep.tile([P, HALF], F32, name="wgt_turned", align_bytes=64)
         wgt_spread = keep.tile([P, S], F32, name="wgt_spread", align_bytes=64)
         nc.vector.memset(wgt_rows[:], 0.0)
-
-        nc.sync.dma_start(offsets[:], offs)
 
         window = [[None] * PACK for a in range(PASSES)]
         for a in range(PASSES):
@@ -78,26 +77,32 @@ def tile_list_heads_tm_res_kernel(tc, xT, w, wgt, r, offs, out):
                     window[a][i] = keep.tile([P, 2 * T], F32, name=f"x{a}{i}", align_bytes=BURST)
                     nc.sync.dma_start(out=window[a][i][:], in_=x_rows[:, i * T : (i + 2) * T])
                 if (a, i) == (0, 0):
-                    nc.sync.dma_start(out=wgt_rows[0:P:GROUP, :], in_=wgt[0:P:GROUP, :])
+                    nc.sync.dma_start(offsets[:], offs)
+                    half_rows = wgt.rearrange("p (h n) -> (p h) n", h=2)
+                    nc.sync.dma_start(out=wgt_rows[0 : P : GROUP // 2, :], in_=half_rows[0 : 2 * P : GROUP + 1, :])
         w_rows = [w[a * K_PASS : (a + 1) * K_PASS, :].rearrange("(p j) n -> p (j n)", j=PACK) for a in range(PASSES)]
         w_sb = [keep.tile([P, PACK * M], F32, name=f"w{a}", align_bytes=BURST) for a in range(PASSES)]
         for a in range(LAST):
             nc.sync.dma_start(out=w_sb[a][:], in_=w_rows[a])
-        for c0, c1 in ((0, 2 * M + N_HALF), (3 * M, 3 * M + N_HALF)):
-            nc.sync.dma_start(out=w_sb[LAST][:, c0:c1], in_=w_rows[LAST][:, c0:c1])
+        nc.sync.dma_start(out=w_sb[LAST][:, : 2 * M], in_=w_rows[LAST][:, : 2 * M])
+        nc.sync.dma_start(
+            out=w_sb[LAST][:].rearrange("p (j n) -> p j n", j=PACK)[:, 2:, :N_HALF],
+            in_=w_rows[LAST].rearrange("p (j n) -> p j n", j=PACK)[:, 2:, :N_HALF],
+        )
         w_rest = keep.tile([P, 2, N_HALF], F32, name="w_rest", align_bytes=BURST)
         nc.sync.dma_start(out=w_rest[:], in_=w_rows[LAST].rearrange("p (j n) -> p j n", j=PACK)[:, 2:, N_HALF:])
-        r_rows = [r[h * HALF : (h + 1) * HALF, :].rearrange("(q e) n -> q (e n)", e=2) for h in range(2)]
-        out_rows = [out[h * HALF : (h + 1) * HALF, :].rearrange("(q e) n -> q (e n)", e=2) for h in range(2)]
-        r_sb = [keep.tile([P, 2 * M], F32, name=f"r{h}", align_bytes=BURST) for h in range(2)]
-        nc.sync.dma_start(out=r_sb[0][:], in_=r_rows[0])
-        for e in range(2):
-            nc.sync.dma_start(out=r_sb[1][:, e * M : (e + 1) * M], in_=r_rows[1][:, e * M : (e + 1) * M])
+        r_rows = r.rearrange("(q b) n -> q (b n)", b=4)
+        out_all = out.rearrange("(q b) n -> q (b n)", b=4)
+        out_rows = [out_all[:, h * 2 * M : (h + 1) * 2 * M] for h in range(2)]
+        r_all = keep.tile([P, 4 * M], F32, name="r_all", align_bytes=BURST)
+        for c0, c1 in ((0, M + N_HALF), (M + N_HALF, 2 * M + N_HALF), (2 * M + N_HALF, 4 * M)):
+            nc.sync.dma_start(out=r_all[:, c0:c1], in_=r_rows[:, c0:c1])
+        r_sb = [r_all[:, h * 2 * M : (h + 1) * 2 * M] for h in range(2)]
 
         nc.vector.transpose(wgt_turned[:], wgt_rows[:])
         nc.vector.tensor_copy(
-            out=wgt_spread[:].rearrange("p (c i) -> p c i", i=GROUP),
-            in_=wgt_turned[:].rearrange("p (c i) -> p c i", i=GROUP)[:, :, 0:1].to_broadcast([P, S // GROUP, GROUP]),
+            out=wgt_spread[:].rearrange("p (h c i) -> p h c i", h=2, i=GROUP),
+            in_=wgt_turned[:].rearrange("p (c h i) -> p h c i", h=2, i=GROUP // 2)[:, :, :, 0:1].to_broadcast([P, 2, HALF // GROUP, GROUP]),
         )
         nc.vector.transpose(wgt_sb[:], wgt_spread[:])
 
@@ -106,11 +111,11 @@ def tile_list_heads_tm_res_kernel(tc, xT, w, wgt, r, offs, out):
         for piece in SHARED_BANK:
             acc[piece] = acc_last[:, piece[2] : piece[3]]
 
-        x_codes = [[keep.tile([P, HALF], U32, name=f"xcodes{a}{h}", align_bytes=64) for h in range(2)] for a in range(LAST)]
-        x_codes.append([keep.tile([P, HALF], U32, name="xcodes_last0", align_bytes=64), work.tile([P, HALF], U32, name="xcodes_last1", offset=0, align_bytes=64)])
-        x_scales = [[keep.tile([P, HALF], U8, name=f"xscales{a}{h}", align_bytes=64) for h in range(2)] for a in range(PASSES)]
+        x_codes = [keep.tile([P, S], U32, name=f"xcodes{a}", align_bytes=64) for a in range(LAST)]
+        x_codes.append(work.tile([P, S], U32, name="xcodes_last", offset=0, align_bytes=64))
+        x_scales = [keep.tile([P, S], U8, name=f"xscales{a}", align_bytes=64) for a in range(PASSES)]
         picked = [ring.tile([P, PACK, S], F32, name="picked") for a in range(PASSES)]
-        x_bf = [[ring.tile([P, HALF * PACK], BF16, name=f"xbf{h}", align_bytes=64) for h in range(2)] for a in range(PASSES)]
+        x_bf = [ring.tile([P, S * PACK], BF16, name="xbf", align_bytes=64) for a in range(PASSES)]
 
         def unpair(copy, a, i, c0, c1):
             if window[a][i] is None:
@@ -130,12 +135,12 @@ def tile_list_heads_tm_res_kernel(tc, xT, w, wgt, r, offs, out):
 
         def weave_x(copy, a, h, j0, j1):
             copy(
-                out=x_bf[a][h][:].rearrange("p (e c u j) -> p c j u e", e=2, u=2, j=PACK)[:, :, j0:j1, :, :],
-                in_=picked[a][:, j0:j1, h * HALF : (h + 1) * HALF].rearrange("p j (c u e) -> p c j u e", u=2, e=2),
+                out=x_bf[a][:].rearrange("p (b q j) -> p q j b", b=4, j=PACK)[:, h * P // 2 : (h + 1) * P // 2, j0:j1, :],
+                in_=picked[a][:, j0:j1, h * HALF : (h + 1) * HALF].rearrange("p j (q b) -> p q j b", b=4),
             )
 
-        def quantize_x(a, h):
-            nc.vector.quantize_mx(out=x_codes[a][h][:].bitcast(FP8X4), scales=x_scales[a][h][:], in_=x_bf[a][h][:])
+        def quantize_x(a):
+            nc.vector.quantize_mx(out=x_codes[a][:].bitcast(FP8X4), scales=x_scales[a][:], in_=x_bf[a][:])
 
         for a in range(LAST):
             unpair(on_scalar, a, 1, 0, T)
@@ -147,8 +152,7 @@ def tile_list_heads_tm_res_kernel(tc, xT, w, wgt, r, offs, out):
             gather(a, 3)
             weave_x(on_scalar, a, 0, 0, PACK)
             weave_x(on_scalar if a else on_vector, a, 1, 0, PACK)
-            quantize_x(a, 0)
-            quantize_x(a, 1)
+            quantize_x(a)
         gather(LAST, 0)
         gather(LAST, 1)
         for h in range(2):
@@ -156,8 +160,7 @@ def tile_list_heads_tm_res_kernel(tc, xT, w, wgt, r, offs, out):
         gather(LAST, 2)
         gather(LAST, 3)
         weave_x(on_scalar, LAST, 0, 2, PACK)
-        weave_x(on_scalar, LAST, 1, 2, PACK)
-        quantize_x(LAST, 0)
+        weave_x(on_vector, LAST, 1, 2, PACK)
 
         for a in range(PASSES):
             w_bf = [keep.tile([P, N_HALF * PACK], BF16, name=f"wbf{a}{g}", align_bytes=64) if a or g else None for g in range(2)]
@@ -176,19 +179,21 @@ def tile_list_heads_tm_res_kernel(tc, xT, w, wgt, r, offs, out):
                 weave(on_scalar, w_bf[1][:, extra * PACK :], w_planes[:, :, N_HALF + extra :])
             else:
                 weave_pair(on_scalar, w_bf[1][:], 0, w_planes[:, 0:2, N_HALF:])
-                weave_pair(on_scalar, w_bf[1][:, NARROW * PACK :], 2, w_rest[:, :, NARROW:])
+                weave_pair(on_scalar, w_bf[1][:, VECTOR_LATE * PACK :], 2, w_rest[:, :, VECTOR_LATE:])
             for g in range(2):
                 width = width0 if g == 0 else N_HALF
                 if (a, g) == (LAST, 1):
-                    weave_pair(on_vector, w_bf[1][:, : NARROW * PACK], 2, w_rest[:, :, :NARROW])
-                for c0 in range(0, N_HALF, width):
+                    weave_pair(on_vector, w_bf[1][:, : VECTOR_LATE * PACK], 2, w_rest[:, :, :VECTOR_LATE])
+                if (a, g) == (LAST, 1):
+                    width = NARROW
+                for c0 in range(0, N_HALF, width) if (a, g) != (LAST, 1) else (NARROW, 0):
                     nc.vector.quantize_mx(
                         out=w_codes[g][:, c0 : c0 + width].bitcast(FP8X4),
                         scales=w_scales[g][:, c0 : c0 + width],
                         in_=w_bf[g][:, c0 * PACK : (c0 + width) * PACK],
                     )
                 if (a, g) == (0, 0):
-                    quantize_x(LAST, 1)
+                    quantize_x(LAST)
             pieces = sorted(OWN_BANK + SHARED_BANK, key=lambda piece: piece[2] // N_HALF)
             sweeps = [(piece, piece[2], piece[3]) for piece in pieces]
             if a == 0:
@@ -198,12 +203,12 @@ def tile_list_heads_tm_res_kernel(tc, xT, w, wgt, r, offs, out):
             for piece, c0, c1 in sweeps:
                 h, e = piece[:2]
                 g = c0 // N_HALF
-                tokens = slice(e * P, (e + 1) * P)
+                tokens = slice((2 * h + e) * P, (2 * h + e + 1) * P)
                 cols = slice(c0 - g * N_HALF, c1 - g * N_HALF)
                 nc.tensor.matmul_mx(
                     out=acc[piece][:, c0 - piece[2] : c1 - piece[2]],
-                    lhsT=x_codes[a][h][:, tokens].bitcast(FP8X4),
-                    lhsT_scale=x_scales[a][h][:, tokens],
+                    lhsT=x_codes[a][:, tokens].bitcast(FP8X4),
+                    lhsT_scale=x_scales[a][:, tokens],
                     rhs=w_codes[g][:, cols].bitcast(FP8X4),
                     rhs_scale=w_scales[g][:, cols],
                     start=a == 0 and c0 == piece[2] and piece != SHARED_BANK[1],

@@ -123,7 +123,7 @@ def tile_list_heads_tm_res_kernel(tc, xT, w, wgt, r, offs, out):
             copy(out=window[a][i][:, c0:c1], in_=window[a][i - 1][:, T + c0 : T + c1])
 
         def gather(a, i):
-            parts = 2 if window[a][i].shape[1] > T or i == PACK - 1 else 1
+            parts = 2 if a < LAST or i in (0, PACK - 1) else 1
             for h in range(parts):
                 c0, c1 = h * S // parts, (h + 1) * S // parts
                 nc.vector.tensor_tensor(

@@ -27,12 +27,19 @@ BURST = 256
 
 SCALAR_SHARE_PLANE3 = 1408
 
-VECTOR_EXTRA_W1 = 64
-VECTOR_LATE = 96
-
-GPSIMD_PIECE = (1, 0, 0, N_HALF)
-OWN_BANK = ((0, 0, 0, N_HALF), GPSIMD_PIECE, (0, 1, 0, N_HALF), (0, 0, N_HALF, M), (0, 1, N_HALF, M), (1, 0, N_HALF, M))
-SHARED_BANK = ((1, 1, 0, N_HALF), (1, 1, N_HALF, M))
+VECTOR_W = {(0, 1): 0, (1, 0): 144, (2, 0): 96, (1, 1): 136}
+VECTOR_LATE = 72
+R_LOADS = ((4, 6), (0, 1, 2), (3, 5, 7))
+STORES = ((4,), (6,), (0,), (1, 2), (3, 5), (7,))
+ADD_ORDER = (4, 6, 0, 2, 1, 3, 5, 7)
+GPSIMD_UNIT = 2
+UNIT_ORDER = ((4, 6, 0, 2), (1, 3, 5, 7))
+KIB = 1024
+NARROW_AT = (3 * KIB // 2, 4 * KIB)
+WOVEN_AT = {(1, 0): 2 * KIB, (2, 0): 4 * KIB, (0, 1): 8 * KIB, (1, 1): 2 * KIB}
+LATE_AT = 4 * KIB
+LATE_UNITS = (0, 6, 1, 2)
+W_LAST_AT = 10 * KIB
 
 
 def weave(copy, out, planes):
@@ -42,11 +49,11 @@ def weave(copy, out, planes):
     )
 
 
-def weave_pair(copy, out, j, planes):
-    copy(
-        out=out.rearrange("p (c i j) -> p c j i", i=4, j=PACK)[:, :, j : j + 2, :],
-        in_=planes.rearrange("p j (c i) -> p c j i", i=4),
-    )
+def units_of(rows, units):
+    step = units[1] - units[0] if len(units) > 1 else 1
+    if step == 1:
+        return rows[:, units[0] * N_HALF : (units[-1] + 1) * N_HALF]
+    return rows.rearrange("p (u n) -> p u n", n=N_HALF)[:, units[0] : units[-1] + 1 : step, :]
 
 
 def tile_list_heads_tm_res_kernel(tc, xT, w, wgt, r, offs, out):
@@ -80,24 +87,35 @@ def tile_list_heads_tm_res_kernel(tc, xT, w, wgt, r, offs, out):
                     nc.sync.dma_start(offsets[:], offs)
                     half_rows = wgt.rearrange("p (h n) -> (p h) n", h=2)
                     nc.sync.dma_start(out=wgt_rows[0 : P : GROUP // 2, :], in_=half_rows[0 : 2 * P : GROUP + 1, :])
-        w_rows = [w[a * K_PASS : (a + 1) * K_PASS, :].rearrange("(p j) n -> p (j n)", j=PACK) for a in range(PASSES)]
-        w_sb = [keep.tile([P, PACK * M], F32, name=f"w{a}", align_bytes=BURST) for a in range(PASSES)]
-        for a in range(LAST):
-            nc.sync.dma_start(out=w_sb[a][:], in_=w_rows[a])
-        nc.sync.dma_start(out=w_sb[LAST][:, : 2 * M], in_=w_rows[LAST][:, : 2 * M])
-        nc.sync.dma_start(
-            out=w_sb[LAST][:].rearrange("p (j n) -> p j n", j=PACK)[:, 2:, :N_HALF],
-            in_=w_rows[LAST].rearrange("p (j n) -> p j n", j=PACK)[:, 2:, :N_HALF],
-        )
-        w_rest = keep.tile([P, 2, N_HALF], F32, name="w_rest", align_bytes=BURST)
-        nc.sync.dma_start(out=w_rest[:], in_=w_rows[LAST].rearrange("p (j n) -> p j n", j=PACK)[:, 2:, N_HALF:])
+        w_rows = [w[a * K_PASS : (a + 1) * K_PASS, :].rearrange("(p j) n -> p j n", j=PACK) for a in range(PASSES)]
+        w_first = keep.tile([P, PACK * M], F32, name="w0", align_bytes=BURST)
+        nc.sync.dma_start(out=w_first[:], in_=w_rows[0].rearrange("p j n -> p (j n)"))
+        w_sb = {(0, g): w_first[:].rearrange("p (j n) -> p j n", j=PACK)[:, :, g * N_HALF : (g + 1) * N_HALF] for g in range(2)}
         r_rows = r.rearrange("(q b) n -> q (b n)", b=4)
-        out_all = out.rearrange("(q b) n -> q (b n)", b=4)
-        out_rows = [out_all[:, h * 2 * M : (h + 1) * 2 * M] for h in range(2)]
-        r_all = keep.tile([P, 4 * M], F32, name="r_all", align_bytes=BURST)
-        for c0, c1 in ((0, M + N_HALF), (M + N_HALF, 2 * M + N_HALF), (2 * M + N_HALF, 4 * M)):
-            nc.sync.dma_start(out=r_all[:, c0:c1], in_=r_rows[:, c0:c1])
-        r_sb = [r_all[:, h * 2 * M : (h + 1) * 2 * M] for h in range(2)]
+        out_rows = out.rearrange("(q b) n -> q (b n)", b=4)
+        r_sb = {}
+
+        def load_w(a, g):
+            if (a, g) == (LAST, 1):
+                half = work.tile([P, PACK, N_HALF], F32, name="w_last", offset=W_LAST_AT, align_bytes=BURST)
+            else:
+                half = keep.tile([P, PACK, N_HALF], F32, name=f"w{a}{g}", align_bytes=BURST)
+            nc.sync.dma_start(out=half[:], in_=w_rows[a][:, :, g * N_HALF : (g + 1) * N_HALF])
+            w_sb[a, g] = half[:]
+
+        def load_r(units):
+            part = keep.tile([P, len(units) * N_HALF], F32, name=f"r{units[0]}", align_bytes=BURST)
+            src = units_of(r_rows, units)
+            nc.sync.dma_start(out=part[:] if src.ndim == 2 else part[:].rearrange("p (u n) -> p u n", n=N_HALF), in_=src)
+            for place, u in enumerate(units):
+                r_sb[u] = part[:, place * N_HALF : (place + 1) * N_HALF]
+
+        load_w(1, 0)
+        load_w(2, 0)
+        load_w(1, 1)
+        load_w(2, 1)
+        for units in R_LOADS:
+            load_r(units)
 
         nc.vector.transpose(wgt_turned[:], wgt_rows[:])
         nc.vector.tensor_copy(
@@ -106,13 +124,10 @@ def tile_list_heads_tm_res_kernel(tc, xT, w, wgt, r, offs, out):
         )
         nc.vector.transpose(wgt_sb[:], wgt_spread[:])
 
-        acc = {piece: psum.tile([P, piece[3] - piece[2]], F32, name="acc%d%d_%d" % piece[:3])[:] for piece in OWN_BANK}
-        acc_last = psum.tile([P, M], F32, name="acc_last")
-        for piece in SHARED_BANK:
-            acc[piece] = acc_last[:, piece[2] : piece[3]]
+        acc = [psum.tile([P, N_HALF], F32, name=f"acc{u}") for u in range(8)]
 
         x_codes = [keep.tile([P, S], U32, name=f"xcodes{a}", align_bytes=64) for a in range(LAST)]
-        x_codes.append(work.tile([P, S], U32, name="xcodes_last", offset=0, align_bytes=64))
+        x_codes.append(None)
         x_scales = [keep.tile([P, S], U8, name=f"xscales{a}", align_bytes=64) for a in range(PASSES)]
         picked = [ring.tile([P, PACK, S], F32, name="picked") for a in range(PASSES)]
         x_bf = [ring.tile([P, S * PACK], BF16, name="xbf", align_bytes=64) for a in range(PASSES)]
@@ -162,71 +177,98 @@ def tile_list_heads_tm_res_kernel(tc, xT, w, wgt, r, offs, out):
         weave_x(on_scalar, LAST, 0, 2, PACK)
         weave_x(on_vector, LAST, 1, 2, PACK)
 
-        for a in range(PASSES):
-            w_bf = [keep.tile([P, N_HALF * PACK], BF16, name=f"wbf{a}{g}", align_bytes=64) if a or g else None for g in range(2)]
-            if a == 0:
-                w_bf[0] = work.tile([P, N_HALF * PACK], BF16, name="wbf_first", offset=0, align_bytes=64)
-            w_codes = [keep.tile([P, N_HALF], U32, name=f"wcodes{a}{g}", align_bytes=64) for g in range(2)]
-            w_scales = [keep.tile([P, N_HALF], U8, name=f"wscales{a}{g}", align_bytes=64) for g in range(2)]
-            w_planes = w_sb[a][:].rearrange("p (j n) -> p j n", j=PACK)
-            width0 = N_HALF if a == 1 else NARROW
-            for c0 in range(0, N_HALF, width0):
-                weave(on_vector, w_bf[0][:, c0 * PACK : (c0 + width0) * PACK], w_planes[:, :, c0 : c0 + width0])
-            if a < LAST:
-                extra = VECTOR_EXTRA_W1 * a
-                if extra:
-                    weave(on_vector, w_bf[1][:, : extra * PACK], w_planes[:, :, N_HALF : N_HALF + extra])
-                weave(on_scalar, w_bf[1][:, extra * PACK :], w_planes[:, :, N_HALF + extra :])
-            else:
-                weave_pair(on_scalar, w_bf[1][:], 0, w_planes[:, 0:2, N_HALF:])
-                weave_pair(on_scalar, w_bf[1][:, VECTOR_LATE * PACK :], 2, w_rest[:, :, VECTOR_LATE:])
-            for g in range(2):
-                width = width0 if g == 0 else N_HALF
-                if (a, g) == (LAST, 1):
-                    weave_pair(on_vector, w_bf[1][:, : VECTOR_LATE * PACK], 2, w_rest[:, :, :VECTOR_LATE])
-                if (a, g) == (LAST, 1):
-                    width = NARROW
-                for c0 in range(0, N_HALF, width) if (a, g) != (LAST, 1) else (NARROW, 0):
-                    nc.vector.quantize_mx(
-                        out=w_codes[g][:, c0 : c0 + width].bitcast(FP8X4),
-                        scales=w_scales[g][:, c0 : c0 + width],
-                        in_=w_bf[g][:, c0 * PACK : (c0 + width) * PACK],
-                    )
-                if (a, g) == (0, 0):
-                    quantize_x(LAST)
-            pieces = sorted(OWN_BANK + SHARED_BANK, key=lambda piece: piece[2] // N_HALF)
-            sweeps = [(piece, piece[2], piece[3]) for piece in pieces]
-            if a == 0:
-                sweeps = [
-                    (piece, c0, c0 + NARROW) for c0 in (0, NARROW) for piece in pieces if piece[2] <= c0 < piece[3]
-                ] + [sweep for sweep in sweeps if sweep[1] >= N_HALF]
-            for piece, c0, c1 in sweeps:
-                h, e = piece[:2]
-                g = c0 // N_HALF
-                tokens = slice((2 * h + e) * P, (2 * h + e + 1) * P)
-                cols = slice(c0 - g * N_HALF, c1 - g * N_HALF)
-                nc.tensor.matmul_mx(
-                    out=acc[piece][:, c0 - piece[2] : c1 - piece[2]],
-                    lhsT=x_codes[a][:, tokens].bitcast(FP8X4),
-                    lhsT_scale=x_scales[a][:, tokens],
-                    rhs=w_codes[g][:, cols].bitcast(FP8X4),
-                    rhs_scale=w_scales[g][:, cols],
-                    start=a == 0 and c0 == piece[2] and piece != SHARED_BANK[1],
-                    stop=a == LAST and piece != SHARED_BANK[0],
-                )
+        w_bf, w_codes, w_scales, result = {}, {}, {}, {}
 
-        result = [keep.tile([P, 2 * M], F32, name=f"result{h}", align_bytes=BURST) for h in range(2)]
-        raw = keep.tile([P, N_HALF], F32, name="raw")
-        h, e, c0, c1 = GPSIMD_PIECE
-        cols = slice(e * M + c0, e * M + c1)
-        nc.scalar.copy(out=raw[:], in_=acc[GPSIMD_PIECE])
-        nc.gpsimd.tensor_tensor(result[h][:, cols], raw[:], r_sb[h][:, cols], ADD)
-        for piece in OWN_BANK:
-            if piece != GPSIMD_PIECE:
-                h, e, c0, c1 = piece
-                cols = slice(e * M + c0, e * M + c1)
-                nc.vector.tensor_tensor(result[h][:, cols], acc[piece], r_sb[h][:, cols], ADD)
-                stored = slice(0, M) if h else cols
-                nc.sync.dma_start(out=out_rows[h][:, stored], in_=result[h][:, stored])
-        nc.vector.tensor_tensor(result[1][:, M:], acc_last[:], r_sb[1][:, M:], ADD)
-        nc.sync.dma_start(out=out_rows[1][:, M:], in_=result[1][:, M:])
+        def codes_for(a, g):
+            w_codes[a, g] = keep.tile([P, N_HALF], U32, name=f"wcodes{a}{g}", align_bytes=64)
+            w_scales[a, g] = keep.tile([P, N_HALF], U8, name=f"wscales{a}{g}", align_bytes=64)
+
+        def weave_w(a, g):
+            w_bf[a, g] = work.tile([P, N_HALF * PACK], BF16, name=f"wbf{a}{g}", offset=WOVEN_AT[a, g], align_bytes=64)
+            cut = VECTOR_W[a, g]
+            if cut:
+                weave(on_vector, w_bf[a, g][:, : cut * PACK], w_sb[a, g][:, :, :cut])
+            if cut < N_HALF:
+                weave(on_scalar, w_bf[a, g][:, cut * PACK :], w_sb[a, g][:, :, cut:])
+
+        def weave_late():
+            late = work.tile([P, 4 * N_HALF], F32, name="late", offset=LATE_AT, align_bytes=BURST)
+            woven = late[:, 3 * NARROW : 3 * NARROW + 2 * N_HALF].bitcast(BF16)
+            woven_parts = woven.rearrange("p (h c i j) -> p h c j i", h=2, i=4, j=PACK)
+            late_planes = w_sb[LAST, 1].rearrange("p j (h c i) -> p h c j i", h=2, i=4)
+            cut = VECTOR_LATE // 4
+            on_vector(out=woven_parts[:, :, :cut], in_=late_planes[:, :, :cut])
+            on_scalar(out=woven_parts[:, :, cut:], in_=late_planes[:, :, cut:])
+            result["late"], result["woven"] = late, woven
+
+        def quantize_w(a, g, c0, c1, src):
+            nc.vector.quantize_mx(out=w_codes[a, g][:, c0:c1].bitcast(FP8X4), scales=w_scales[a, g][:, c0:c1], in_=src)
+
+        def quantize_half(a, g):
+            codes_for(a, g)
+            quantize_w(a, g, 0, N_HALF, w_bf[a, g][:])
+
+        def multiply(a, g, u, c0=0, c1=N_HALF):
+            tokens = slice(u // 2 * P, (u // 2 + 1) * P)
+            nc.tensor.matmul_mx(
+                out=acc[u][:, c0:c1],
+                lhsT=x_codes[a][:, tokens].bitcast(FP8X4),
+                lhsT_scale=x_scales[a][:, tokens],
+                rhs=w_codes[a, g][:, c0:c1].bitcast(FP8X4),
+                rhs_scale=w_scales[a, g][:, c0:c1],
+                start=a == 0 and c0 == 0,
+                stop=a == LAST,
+            )
+
+        parts, sums = {}, {}
+
+        def add(u):
+            units = [group for group in STORES if u in group][0]
+            if units not in parts:
+                if units[0] in LATE_UNITS:
+                    first = LATE_UNITS.index(units[0])
+                    parts[units] = late[:, first * N_HALF : (first + len(units)) * N_HALF]
+                else:
+                    parts[units] = keep.tile([P, len(units) * N_HALF], F32, name=f"result{units[0]}", align_bytes=BURST)[:]
+            part = parts[units]
+            slot = units.index(u)
+            sums[u] = part[:, slot * N_HALF : (slot + 1) * N_HALF]
+            if u == GPSIMD_UNIT:
+                raw = work.tile([P, N_HALF], F32, name="raw", offset=W_LAST_AT, align_bytes=BURST)
+                nc.scalar.copy(out=raw[:], in_=acc[u][:])
+                nc.gpsimd.tensor_tensor(sums[u], raw[:], r_sb[u], ADD)
+            else:
+                nc.vector.tensor_tensor(sums[u], acc[u][:], r_sb[u], ADD)
+            if all(v in sums for v in units):
+                dst = units_of(out_rows, units)
+                nc.sync.dma_start(out=dst, in_=part if dst.ndim == 2 else part.rearrange("p (u n) -> p u n", n=N_HALF))
+
+        w_narrow = [work.tile([P, NARROW * PACK], BF16, name=f"wbf_narrow{part}", offset=NARROW_AT[part], align_bytes=64) for part in range(2)]
+        for part in range(2):
+            weave(on_vector, w_narrow[part][:], w_sb[0, 0][:, :, part * NARROW : (part + 1) * NARROW])
+        weave_w(0, 1)
+        codes_for(0, 0)
+        for part in range(2):
+            quantize_w(0, 0, part * NARROW, (part + 1) * NARROW, w_narrow[part][:])
+            for u in UNIT_ORDER[0]:
+                multiply(0, 0, u, part * NARROW, (part + 1) * NARROW)
+        x_codes[LAST] = work.tile([P, S], U32, name="xcodes_last", offset=0, align_bytes=64)
+        quantize_x(LAST)
+        halves = ((0, 1), (1, 0), (LAST, 0), (1, 1))
+        for (a, g), ahead in zip(halves, halves[1:] + (None,)):
+            if ahead:
+                weave_w(*ahead)
+            quantize_half(a, g)
+            for u in UNIT_ORDER[g]:
+                multiply(a, g, u)
+
+        weave_late()
+        late, woven = result["late"], result["woven"]
+        add(ADD_ORDER[0])
+        codes_for(LAST, 1)
+        for part in range(2):
+            quantize_w(LAST, 1, part * NARROW, (part + 1) * NARROW, woven[:, part * NARROW * PACK : (part + 1) * NARROW * PACK])
+        for u in UNIT_ORDER[1]:
+            multiply(LAST, 1, u)
+        for u in ADD_ORDER[1:]:
+            add(u)

@@ -138,7 +138,7 @@ def tile_list_heads_tm_res_kernel(tc, xT, w, wgt, r, offs, out):
             copy(out=window[a][i][:, c0:c1], in_=window[a][i - 1][:, T + c0 : T + c1])
 
         def gather(a, i):
-            parts = 2 if a < LAST or i in (0, PACK - 1) else 1
+            parts = 1 if (a, i) == (LAST, 2) else 2
             for h in range(parts):
                 c0, c1 = h * S // parts, (h + 1) * S // parts
                 nc.vector.tensor_tensor(

from contextlib import ExitStack

import concourse.mybir as mybir

K, M, T, S = 1536, 512, 2048, 512
FLOPS = 2 * K * M * S

F32 = mybir.dt.float32
BF16 = mybir.dt.bfloat16
U32 = mybir.dt.uint32
U16 = mybir.dt.uint16
U8 = mybir.dt.uint8
FP8X4 = mybir.dt.float8_e4m3fn_x4
MULT = mybir.AluOpType.mult
ADD = mybir.AluOpType.add

P = 128
PACK = 4
K_PASS = P * PACK
PASSES = K // K_PASS
LAST = PASSES - 1
GROUP = 16
HALF = S // 2
N_HALF = M // 2
NARROW = N_HALF // 2
BURST = 256

SCALAR_SHARE_PLANE3 = 1408

VECTOR_W = {(0, 1): 0, (1, 0): 144, (2, 0): 96, (1, 1): 136}
VECTOR_LATE = 72
R_LOADS = ((4, 6), (0, 1, 2), (3, 5, 7))
STORES = ((4,), (6,), (0,), (1, 2), (3, 5), (7,))
ADD_ORDER = (4, 6, 0, 2, 1, 3, 5, 7)
GPSIMD_UNIT = 2
UNIT_ORDER = ((4, 6, 0, 2), (1, 3, 5, 7))
KIB = 1024
NARROW_AT = (3 * KIB // 2, 4 * KIB)
WOVEN_AT = {(1, 0): 2 * KIB, (2, 0): 4 * KIB, (0, 1): 8 * KIB, (1, 1): 2 * KIB}
LATE_AT = 4 * KIB
LATE_UNITS = (0, 6, 1, 2)
W_LAST_AT = 10 * KIB


def weave(copy, out, planes):
    copy(
        out=out.rearrange("p (c i j) -> p c j i", i=4, j=PACK),
        in_=planes.rearrange("p j (c i) -> p c j i", i=4),
    )


def units_of(rows, units):
    step = units[1] - units[0] if len(units) > 1 else 1
    if step == 1:
        return rows[:, units[0] * N_HALF : (units[-1] + 1) * N_HALF]
    return rows.rearrange("p (u n) -> p u n", n=N_HALF)[:, units[0] : units[-1] + 1 : step, :]


def tile_list_heads_tm_res_kernel(tc, xT, w, wgt, r, offs, out):
    nc = tc.nc
    on_scalar, on_vector = nc.scalar.copy, nc.vector.tensor_copy
    with ExitStack() as ctx:
        keep = ctx.enter_context(tc.tile_pool(name="keep", bufs=1))
        ring = ctx.enter_context(tc.tile_pool(name="ring", bufs=2))
        work = ctx.enter_context(tc.tile_pool(name="work", bufs=1))
        psum = ctx.enter_context(tc.psum_pool(name="psum", bufs=1))

        offsets = keep.tile([P, S // GROUP], U16, name="offsets", align_bytes=BURST)
        wgt_sb = keep.tile([P, S], F32, name="wgt_sb", align_bytes=64)
        wgt_rows = keep.tile([P, HALF], F32, name="wgt_rows", align_bytes=BURST)
        wgt_turned = keep.tile([P, HALF], F32, name="wgt_turned", align_bytes=64)
        wgt_spread = keep.tile([P, S], F32, name="wgt_spread", align_bytes=64)
        nc.vector.memset(wgt_rows[:], 0.0)

        window = [[None] * PACK for a in range(PASSES)]
        for a in range(PASSES):
            x_rows = xT[a * K_PASS : (a + 1) * K_PASS, :].rearrange("(p j) t -> p (j t)", j=PACK)
            for i in range(0, PACK, 2):
                if a == LAST:
                    for e in (i, i + 1):
                        window[a][e] = keep.tile([P, T], F32, name=f"x{a}{e}", align_bytes=BURST)
                        nc.sync.dma_start(out=window[a][e][:], in_=x_rows[:, e * T : (e + 1) * T])
                else:
                    window[a][i] = keep.tile([P, 2 * T], F32, name=f"x{a}{i}", align_bytes=BURST)
                    nc.sync.dma_start(out=window[a][i][:], in_=x_rows[:, i * T : (i + 2) * T])
                if (a, i) == (0, 0):
                    nc.sync.dma_start(offsets[:], offs)
                    half_rows = wgt.rearrange("p (h n) -> (p h) n", h=2)
                    nc.sync.dma_start(out=wgt_rows[0 : P : GROUP // 2, :], in_=half_rows[0 : 2 * P : GROUP + 1, :])
        w_rows = [w[a * K_PASS : (a + 1) * K_PASS, :].rearrange("(p j) n -> p j n", j=PACK) for a in range(PASSES)]
        w_first = keep.tile([P, PACK * M], F32, name="w0", align_bytes=BURST)
        nc.sync.dma_start(out=w_first[:], in_=w_rows[0].rearrange("p j n -> p (j n)"))
        w_sb = {(0, g): w_first[:].rearrange("p (j n) -> p j n", j=PACK)[:, :, g * N_HALF : (g + 1) * N_HALF] for g in range(2)}
        r_rows = r.rearrange("(q b) n -> q (b n)", b=4)
        out_rows = out.rearrange("(q b) n -> q (b n)", b=4)
        r_sb = {}

        def load_w(a, g):
            if (a, g) == (LAST, 1):
                half = work.tile([P, PACK, N_HALF], F32, name="w_last", offset=W_LAST_AT, align_bytes=BURST)
            else:
                half = keep.tile([P, PACK, N_HALF], F32, name=f"w{a}{g}", align_bytes=BURST)
            nc.sync.dma_start(out=half[:], in_=w_rows[a][:, :, g * N_HALF : (g + 1) * N_HALF])
            w_sb[a, g] = half[:]

        def load_r(units):
            part = keep.tile([P, len(units) * N_HALF], F32, name=f"r{units[0]}", align_bytes=BURST)
            src = units_of(r_rows, units)
            nc.sync.dma_start(out=part[:] if src.ndim == 2 else part[:].rearrange("p (u n) -> p u n", n=N_HALF), in_=src)
            for place, u in enumerate(units):
                r_sb[u] = part[:, place * N_HALF : (place + 1) * N_HALF]

        load_w(1, 0)
        load_w(2, 0)
        load_w(1, 1)
        load_w(2, 1)
        for units in R_LOADS:
            load_r(units)

        nc.vector.transpose(wgt_turned[:], wgt_rows[:])
        nc.vector.tensor_copy(
            out=wgt_spread[:].rearrange("p (h c i) -> p h c i", h=2, i=GROUP),
            in_=wgt_turned[:].rearrange("p (c h i) -> p h c i", h=2, i=GROUP // 2)[:, :, :, 0:1].to_broadcast([P, 2, HALF // GROUP, GROUP]),
        )
        nc.vector.transpose(wgt_sb[:], wgt_spread[:])

        acc = [psum.tile([P, N_HALF], F32, name=f"acc{u}") for u in range(8)]

        x_codes = [keep.tile([P, S], U32, name=f"xcodes{a}", align_bytes=64) for a in range(LAST)]
        x_codes.append(None)
        x_scales = [keep.tile([P, S], U8, name=f"xscales{a}", align_bytes=64) for a in range(PASSES)]
        picked = [ring.tile([P, PACK, S], F32, name="picked") for a in range(PASSES)]
        x_bf = [ring.tile([P, S * PACK], BF16, name="xbf", align_bytes=64) for a in range(PASSES)]

        def unpair(copy, a, i, c0, c1):
            if window[a][i] is None:
                window[a][i] = ring.tile([P, T], F32, name="second")
            copy(out=window[a][i][:, c0:c1], in_=window[a][i - 1][:, T + c0 : T + c1])

        def gather(a, i):
            parts = 1 if (a, i) == (LAST, 2) else 2
            for h in range(parts):
                c0, c1 = h * S // parts, (h + 1) * S // parts
                nc.vector.tensor_tensor(
                    picked[a][:, i, c0:c1],
                    window[a][i][:].indirect(offsets[:, c0 // GROUP : c1 // GROUP]),
                    wgt_sb[:, c0:c1],
                    MULT,
                )

        def weave_x(copy, a, h, j0, j1):
            copy(
                out=x_bf[a][:].rearrange("p (b q j) -> p q j b", b=4, j=PACK)[:, h * P // 2 : (h + 1) * P // 2, j0:j1, :],
                in_=picked[a][:, j0:j1, h * HALF : (h + 1) * HALF].rearrange("p j (q b) -> p q j b", b=4),
            )

        def quantize_x(a):
            nc.vector.quantize_mx(out=x_codes[a][:].bitcast(FP8X4), scales=x_scales[a][:], in_=x_bf[a][:])

        for a in range(LAST):
            unpair(on_scalar, a, 1, 0, T)
            gather(a, 0)
            gather(a, 1)
            unpair(on_scalar, a, 3, 0, SCALAR_SHARE_PLANE3)
            gather(a, 2)
            unpair(on_vector, a, 3, SCALAR_SHARE_PLANE3, T)
            gather(a, 3)
            weave_x(on_scalar, a, 0, 0, PACK)
            weave_x(on_scalar if a else on_vector, a, 1, 0, PACK)
            quantize_x(a)
        gather(LAST, 0)
        gather(LAST, 1)
        for h in range(2):
            weave_x(on_scalar, LAST, h, 0, 2)
        gather(LAST, 2)
        gather(LAST, 3)
        weave_x(on_scalar, LAST, 0, 2, PACK)
        weave_x(on_vector, LAST, 1, 2, PACK)

        w_bf, w_codes, w_scales, result = {}, {}, {}, {}

        def codes_for(a, g):
            w_codes[a, g] = keep.tile([P, N_HALF], U32, name=f"wcodes{a}{g}", align_bytes=64)
            w_scales[a, g] = keep.tile([P, N_HALF], U8, name=f"wscales{a}{g}", align_bytes=64)

        def weave_w(a, g):
            w_bf[a, g] = work.tile([P, N_HALF * PACK], BF16, name=f"wbf{a}{g}", offset=WOVEN_AT[a, g], align_bytes=64)
            cut = VECTOR_W[a, g]
            if cut:
                weave(on_vector, w_bf[a, g][:, : cut * PACK], w_sb[a, g][:, :, :cut])
            if cut < N_HALF:
                weave(on_scalar, w_bf[a, g][:, cut * PACK :], w_sb[a, g][:, :, cut:])

        def weave_late():
            late = work.tile([P, 4 * N_HALF], F32, name="late", offset=LATE_AT, align_bytes=BURST)
            woven = late[:, 3 * NARROW : 3 * NARROW + 2 * N_HALF].bitcast(BF16)
            woven_parts = woven.rearrange("p (h c i j) -> p h c j i", h=2, i=4, j=PACK)
            late_planes = w_sb[LAST, 1].rearrange("p j (h c i) -> p h c j i", h=2, i=4)
            cut = VECTOR_LATE // 4
            on_vector(out=woven_parts[:, :, :cut], in_=late_planes[:, :, :cut])
            on_scalar(out=woven_parts[:, :, cut:], in_=late_planes[:, :, cut:])
            result["late"], result["woven"] = late, woven

        def quantize_w(a, g, c0, c1, src):
            nc.vector.quantize_mx(out=w_codes[a, g][:, c0:c1].bitcast(FP8X4), scales=w_scales[a, g][:, c0:c1], in_=src)

        def quantize_half(a, g):
            codes_for(a, g)
            quantize_w(a, g, 0, N_HALF, w_bf[a, g][:])

        def multiply(a, g, u, c0=0, c1=N_HALF):
            tokens = slice(u // 2 * P, (u // 2 + 1) * P)
            nc.tensor.matmul_mx(
                out=acc[u][:, c0:c1],
                lhsT=x_codes[a][:, tokens].bitcast(FP8X4),
                lhsT_scale=x_scales[a][:, tokens],
                rhs=w_codes[a, g][:, c0:c1].bitcast(FP8X4),
                rhs_scale=w_scales[a, g][:, c0:c1],
                start=a == 0 and c0 == 0,
                stop=a == LAST,
            )

        parts, sums = {}, {}

        def add(u):
            units = [group for group in STORES if u in group][0]
            if units not in parts:
                if units[0] in LATE_UNITS:
                    first = LATE_UNITS.index(units[0])
                    parts[units] = late[:, first * N_HALF : (first + len(units)) * N_HALF]
                else:
                    parts[units] = keep.tile([P, len(units) * N_HALF], F32, name=f"result{units[0]}", align_bytes=BURST)[:]
            part = parts[units]
            slot = units.index(u)
            sums[u] = part[:, slot * N_HALF : (slot + 1) * N_HALF]
            if u == GPSIMD_UNIT:
                raw = work.tile([P, N_HALF], F32, name="raw", offset=W_LAST_AT, align_bytes=BURST)
                nc.scalar.copy(out=raw[:], in_=acc[u][:])
                nc.gpsimd.tensor_tensor(sums[u], raw[:], r_sb[u], ADD)
            else:
                nc.vector.tensor_tensor(sums[u], acc[u][:], r_sb[u], ADD)
            if all(v in sums for v in units):
                dst = units_of(out_rows, units)
                nc.sync.dma_start(out=dst, in_=part if dst.ndim == 2 else part.rearrange("p (u n) -> p u n", n=N_HALF))

        w_narrow = [work.tile([P, NARROW * PACK], BF16, name=f"wbf_narrow{part}", offset=NARROW_AT[part], align_bytes=64) for part in range(2)]
        for part in range(2):
            weave(on_vector, w_narrow[part][:], w_sb[0, 0][:, :, part * NARROW : (part + 1) * NARROW])
        weave_w(0, 1)
        codes_for(0, 0)
        for part in range(2):
            quantize_w(0, 0, part * NARROW, (part + 1) * NARROW, w_narrow[part][:])
            for u in UNIT_ORDER[0]:
                multiply(0, 0, u, part * NARROW, (part + 1) * NARROW)
        x_codes[LAST] = work.tile([P, S], U32, name="xcodes_last", offset=0, align_bytes=64)
        quantize_x(LAST)
        halves = ((0, 1), (1, 0), (LAST, 0), (1, 1))
        for (a, g), ahead in zip(halves, halves[1:] + (None,)):
            if ahead:
                weave_w(*ahead)
            quantize_half(a, g)
            for u in UNIT_ORDER[g]:
                multiply(a, g, u)

        weave_late()
        late, woven = result["late"], result["woven"]
        add(ADD_ORDER[0])
        codes_for(LAST, 1)
        for part in range(2):
            quantize_w(LAST, 1, part * NARROW, (part + 1) * NARROW, woven[:, part * NARROW * PACK : (part + 1) * NARROW * PACK])
        for u in UNIT_ORDER[1]:
            multiply(LAST, 1, u)
        for u in ADD_ORDER[1:]:
            add(u)
